import numpy as np
import ml_dtypes


def mxq(x, axis, fmt="e4m3"):
    dtype, down = {"e4m3": (ml_dtypes.float8_e4m3fn, 7), "e5m2": (ml_dtypes.float8_e5m2, 14)}[fmt]
    v = np.moveaxis(np.asarray(x, np.float32).astype(ml_dtypes.bfloat16).astype(np.float64), axis, -1)
    blocks = v.reshape(v.shape[:-1] + (-1, 32))
    amax = np.abs(blocks).max(-1, keepdims=True)
    byte = np.maximum(np.where(amax > 0, np.frexp(amax)[1] - 1 + 127, 0) - down, 1)
    scale = np.exp2(byte - 127.0)
    codes = (blocks / scale).astype(np.float32).astype(dtype).astype(np.float64)
    return np.moveaxis((codes * scale).reshape(v.shape), -1, axis)


WIDE = False


def mx_kscale(k, group=512):
    if not WIDE:
        return np.ones(k)
    levels = np.array([10, -10, 5, -5, 0])
    if group != 512:
        return np.exp2(np.random.permutation(np.resize(levels, k // group))).repeat(group)
    if k % 512:
        return np.exp2(np.random.permutation(np.resize(levels, k // 32))).repeat(32)
    a = np.empty((k // 512, 16))
    for p in range(k // 512):
        a[p, :8] = np.random.permutation(np.resize(levels, 8))
        for g in range(8):
            far = levels[np.abs(levels - a[p, g]) >= 10]
            a[p, g + 8] = far[np.random.randint(len(far))]
    return np.exp2(a.ravel()).repeat(32)


def f64(x):
    return np.asarray(x).astype(np.float64)


def striped(idx):
    return np.tile(np.asarray(idx).reshape(-1, 16).T, (8, 1)).astype(np.uint16)


def unstriped(offs):
    return offs[:16].T.reshape(-1).astype(np.int64)


H, KV, D, NQ, N = 4, 4, 128, 512, 1024


def setup_inputs():
    n = np.random.standard_normal
    s = mx_kscale(D, 0)[:, None]
    u = mx_kscale(N)
    t = np.random.uniform(0.5, 2.0, N) * u
    v = n((KV, N, 128))
    v[:, :, 127] = 1.0
    return {
        "qT": (n((H, D, NQ)) * s * (0.70 / np.sqrt(D))).astype(np.float32),
        "kT": (n((KV, D, N)) / s).astype(np.float32),
        "t": t.reshape(N, 1).astype(np.float32),
        "v": (v / t[:, None]).astype(np.float32),
    }


def reference(qT, kT, t, v):
    a = mxq(f64(kT), 1, "e4m3").transpose(0, 2, 1) @ mxq(f64(qT), 1, "e4m3")
    p = np.square(np.maximum(a, 0.0))
    w = p * f64(t)
    y = mxq(w, 1, "e4m3").transpose(0, 2, 1) @ mxq(f64(v), 1, "e4m3")
    y = y / (y[:, :, 127:128] + 1.0)
    return y

@@ -1,0 +1,284 @@
+from contextlib import ExitStack
+
+import concourse.mybir as mybir
+
+H, D, NQ, N = 4, 128, 512, 1024
+FLOPS = 2 * 2 * H * D * NQ * N
+
+F32 = mybir.dt.float32
+BF16 = mybir.dt.bfloat16
+U32 = mybir.dt.uint32
+U8 = mybir.dt.uint8
+X4 = mybir.dt.float8_e4m3fn_x4
+ALU = mybir.AluOpType
+ACT = mybir.ActivationFunctionType
+
+P = 128
+PACK = 4
+ROWS = 32
+QB = 128
+NQB = NQ // QB
+PASS = P * PACK
+NPASS = N // PASS
+HALF = PASS // 2
+BANK = 512
+STEPS = NPASS * NQB
+X_BUFS = 8
+W_BUFS = 3
+TINY = 2.0 ** -126
+
+
+def tile_rows_relu2_kernel(tc, qT, kT, t, v, out):
+    nc = tc.nc
+    with ExitStack() as ctx:
+        sb = ctx.enter_context(tc.tile_pool(name="sb", bufs=1))
+        ps = ctx.enter_context(tc.psum_pool(name="ps", bufs=1))
+        ctx.enter_context(tc.manual_schedule())
+
+        def tiles(name, count, width, dtype):
+            return [sb.tile([P, width], dtype, name="%s%d" % (name, i), align_bytes=64) for i in range(count)]
+
+        def planes(name, count, words):
+            return list(zip(tiles(name + "_codes", count, words, U32), tiles(name + "_scales", count, words, U8)))
+
+        q_hbm = qT.rearrange("h (p j) n -> (h p) j n", j=PACK)
+        k_hbm = kT.rearrange("h (p j) n -> (h p) j n", j=PACK)
+
+        q_raw = tiles("q_raw", 2, PACK * QB, F32) + tiles("q_raw_rest", 1, PACK * 2 * QB, F32)
+        k_raw = tiles("k_raw", 2 * NPASS, PACK * HALF, F32)
+        v_raw = tiles("v_raw", H, NPASS * PACK * D, F32)
+        q_stage = tiles("q_stage", 2, PACK * QB, BF16)
+        k_stage0 = tiles("k_stage_first", 4, 2 * HALF, BF16)
+        k_stage1 = tiles("k_stage_second", 1, PACK * PASS, BF16)[0]
+        w_stage = tiles("w_stage", W_BUFS, H * BANK, BF16)
+        x_buf = tiles("x_buf", X_BUFS, BANK, F32)
+        q_mx = planes("q", NQB, QB)
+        k_mx = planes("k", NPASS, PASS)
+        v_mx = planes("v", H, NPASS * D)
+        w_mx = planes("w", STEPS, H * QB)
+        t_raw, t_abs, t_safe, r0, s0, corr, t_root, t_pos, t_sign = tiles("t_col", 9, NPASS * PACK, F32)
+        den = tiles("den", NQB + 1, H, F32)
+        rec = tiles("rec", NQB + 1, H, F32)
+        o_buf = tiles("o_buf", NQB, H * D, F32)
+        o_last = tiles("o_last", 1, D, F32)[0]
+        score = [ps.tile([P, BANK], F32, name="score%d" % g) for g in range(H)]
+        y_bank = [ps.tile([P, BANK], F32, name="y%d" % b) for b in range(4)]
+
+        def load_q(tile, first, width):
+            nc.sync.dma_start(out=tile[:].rearrange("p (j n) -> p j n", j=PACK), in_=q_hbm[:, :, first : first + width])
+
+        def load_k(half):
+            nc.sync.dma_start(
+                out=k_raw[half][:].rearrange("p (j n) -> p j n", j=PACK), in_=k_hbm[:, :, half * HALF : (half + 1) * HALF]
+            )
+
+        def load_v(g):
+            nc.sync.dma_start(
+                out=v_raw[g][:].rearrange("p (c x) -> p c x", c=NPASS),
+                in_=v[g].rearrange("(c p j) e -> p c (j e)", c=NPASS, j=PACK),
+            )
+
+        def walk_src(rows):
+            return rows.rearrange("p j (u i) -> p u j i", i=PACK)
+
+        def walk_dst(flat):
+            return flat.rearrange("p (u i j) -> p u j i", i=PACK, j=PACK)
+
+        def q_rows(b):
+            if b < 2:
+                return q_raw[b][:].rearrange("p (j n) -> p j n", j=PACK)
+            return q_raw[2][:].rearrange("p (j n) -> p j n", j=PACK)[:, :, (b - 2) * QB : (b - 1) * QB]
+
+        def k_src(half, pair):
+            return k_raw[half][:].rearrange("p (j s r) -> p s j r", j=PACK, r=PACK)[:, :, :, 2 * pair : 2 * pair + 2]
+
+        def quantize(mx, first, stage):
+            words = stage.shape[1] // PACK
+            nc.vector.quantize_mx(
+                out=mx[0][:, first : first + words].bitcast(X4), scales=mx[1][:, first : first + words], in_=stage
+            )
+
+        def mm(dst, lhs, lrows, lcol, rhs, rrows, rcol, start, stop):
+            nc.tensor.matmul_mx(
+                out=dst,
+                lhsT=lhs[0][lrows, lcol : lcol + P].bitcast(X4),
+                lhsT_scale=lhs[1][lrows, lcol : lcol + P],
+                rhs=rhs[0][rrows, rcol : rcol + P].bitcast(X4),
+                rhs_scale=rhs[1][rrows, rcol : rcol + P],
+                start=start,
+                stop=stop,
+            )
+
+        def scores(step, heads):
+            c, b = divmod(step, NQB)
+            for r in range(PACK):
+                for g in heads:
+                    rows = slice(ROWS * g, ROWS * (g + 1))
+                    mm(score[g][:, r * QB : (r + 1) * QB], k_mx[c], rows, r * P, q_mx[b], rows, 0, True, True)
+
+        def relu_scale(step, g):
+            c = step // NQB
+            nc.vector.scalar_tensor_tensor(
+                out=x_buf[(step * H + g) % X_BUFS][:].rearrange("p (n r) -> p n r", r=PACK),
+                in0=score[g][:].rearrange("p (r n) -> p n r", r=PACK),
+                scalar=0.0,
+                in1=t_root[:, c * PACK : (c + 1) * PACK].unsqueeze(1).to_broadcast([P, QB, PACK]),
+                op0=ALU.max,
+                op1=ALU.mult,
+            )
+
+        def square(step, g):
+            nc.scalar.activation(
+                out=w_stage[step % W_BUFS][:, g * BANK : (g + 1) * BANK],
+                in_=x_buf[(step * H + g) % X_BUFS][:],
+                func=ACT.Square,
+            )
+
+        def v_stage(g):
+            return w_stage[g % W_BUFS][:, 0 : NPASS * PACK * D]
+
+        def cast_v(g):
+            for c in range(NPASS):
+                cols = slice(c * PACK * D, (c + 1) * PACK * D)
+                nc.gpsimd.tensor_tensor(
+                    out=walk_dst(v_stage(g)[:, cols]),
+                    in0=walk_src(v_raw[g][:, cols].rearrange("p (j e) -> p j e", j=PACK)),
+                    in1=t_sign[:, c * PACK : (c + 1) * PACK].unsqueeze(1).unsqueeze(3).to_broadcast([P, D // PACK, PACK, PACK]),
+                    op=ALU.mult,
+                )
+
+        def second(b, g, dst, passes):
+            for c in passes:
+                mm(dst, w_mx[c * NQB + b], slice(0, P), g * QB, v_mx[g], slice(0, P), c * D, c == 0, c == NPASS - 1)
+
+        def den_add(slot, bank, count):
+            nc.vector.tensor_scalar(
+                out=den[slot][:, 0:count],
+                in0=bank[:].rearrange("p (g e) -> p g e", e=D)[:, 0:count, D - 1],
+                scalar1=1.0,
+                scalar2=None,
+                op0=ALU.add,
+            )
+
+        def den_rec(slot, count):
+            nc.vector.reciprocal(out=rec[slot][:, 0:count], in_=den[slot][:, 0:count])
+
+        def normalise(b, bank, count):
+            for g in range(count):
+                cols = slice(g * D, (g + 1) * D)
+                nc.scalar.activation(out=o_buf[b][:, cols], in_=bank[:, cols], func=ACT.Copy, scale=rec[b][:, g : g + 1])
+            nc.sync.dma_start(
+                out=out[0:count, b * QB : (b + 1) * QB, :].rearrange("g m e -> m g e"),
+                in_=o_buf[b][:, 0 : count * D].rearrange("p (g e) -> p g e", e=D),
+            )
+
+        nc.scalar.dma_start(
+            out=t_raw[:].rearrange("p (c j) -> p c j", c=NPASS), in_=t.rearrange("(c p j) o -> p c (j o)", c=NPASS, j=PACK)
+        )
+        load_q(q_raw[0], 0, QB)
+        load_k(0)
+        load_k(1)
+        load_q(q_raw[1], QB, QB)
+        load_q(q_raw[2], 2 * QB, 2 * QB)
+        load_k(2)
+        load_k(3)
+        for g in range(H):
+            load_v(g)
+
+        nc.vector.scalar_tensor_tensor(out=t_abs[:], in0=t_raw[:], scalar=-1.0, in1=t_raw[:], op0=ALU.mult, op1=ALU.max)
+        nc.vector.tensor_scalar(out=t_safe[:], in0=t_abs[:], scalar1=TINY, scalar2=None, op0=ALU.max)
+        nc.scalar.activation(out=r0[:], in_=t_safe[:], func=ACT.Abs_reciprocal_sqrt)
+        nc.gpsimd.tensor_scalar(out=t_pos[:], in0=t_raw[:], scalar1=0.0, scalar2=2.0, op0=ALU.is_ge, op1=ALU.mult)
+        nc.gpsimd.tensor_scalar(out=t_sign[:], in0=t_pos[:], scalar1=1.0, scalar2=-1.0, op0=ALU.mult, op1=ALU.add)
+        nc.scalar.copy(out=walk_dst(q_stage[0][:]), in_=walk_src(q_rows(0)))
+        nc.vector.tensor_tensor(out=s0[:], in0=t_abs[:], in1=r0[:], op=ALU.mult)
+
+        def first_k_dst(half, pair):
+            return k_stage0[2 * half + pair][:].rearrange("p (r s j) -> p s j r", r=2, j=PACK)
+
+        def first_k_quantize(half, pair):
+            for rr in range(2):
+                quantize(k_mx[0], (2 * pair + rr) * P + half * (P // 2), k_stage0[2 * half + pair][:, rr * HALF : (rr + 1) * HALF])
+
+        nc.vector.tensor_copy(out=first_k_dst(0, 0), in_=k_src(0, 0))
+        nc.scalar.copy(out=first_k_dst(0, 1), in_=k_src(0, 1))
+        nc.vector.scalar_tensor_tensor(out=corr[:], in0=s0[:], scalar=-0.5, in1=r0[:], op0=ALU.mult, op1=ALU.mult)
+        quantize(q_mx[0], 0, q_stage[0][:])
+        nc.vector.scalar_tensor_tensor(out=t_root[:], in0=corr[:], scalar=1.5, in1=s0[:], op0=ALU.add, op1=ALU.mult)
+        first_k_quantize(0, 0)
+        first_k_quantize(0, 1)
+        nc.vector.tensor_copy(out=first_k_dst(1, 0), in_=k_src(1, 0))
+        nc.scalar.copy(out=first_k_dst(1, 1), in_=k_src(1, 1))
+        first_k_quantize(1, 0)
+        first_k_quantize(1, 1)
+        scores(0, (0, 1))
+        scores(0, (2, 3))
+        nc.scalar.copy(out=walk_dst(q_stage[1][:]), in_=walk_src(q_rows(1)))
+
+        def cast_second_k(piece):
+            half, pair = divmod(piece, 2)
+            dst = k_stage1[:].rearrange("p (r s j) -> p s j r", r=PACK, j=PACK)
+            nc.scalar.copy(
+                out=dst[:, half * (P // 2) : (half + 1) * (P // 2), :, 2 * pair : 2 * pair + 2], in_=k_src(2 + half, pair)
+            )
+
+        second_k_pieces = {0: (0,), 1: (1, 2), 2: (3,)}
+        last = STEPS - 1
+        for step in range(STEPS):
+            for g in (0, 1):
+                relu_scale(step, g)
+                square(step, g)
+                if g == 0 and step - 2 - NQB >= 0:
+                    den_rec(step - 2 - NQB, H)
+            if step + 1 < NQB:
+                quantize(q_mx[step + 1], 0, q_stage[1 if step < 2 else 0][:])
+            if step + 1 == NQB:
+                quantize(k_mx[1], 0, k_stage1[:])
+            if step < last:
+                scores(step + 1, (0, 1))
+            if 2 <= step < 2 + H:
+                quantize(v_mx[step - 2], 0, v_stage(step - 2))
+            if step >= 1:
+                quantize(w_mx[step - 1], 0, w_stage[(step - 1) % W_BUFS][:])
+            if step == 0:
+                for b in (2, 3):
+                    nc.gpsimd.tensor_scalar(
+                        out=walk_dst(q_stage[3 - b][:]), in0=walk_src(q_rows(b)), scalar1=1.0, scalar2=0.0, op0=ALU.mult, op1=ALU.add
+                    )
+            if 1 <= step < 1 + H:
+                cast_v(step - 1)
+            done = step - 1 - NQB
+            if done >= 0:
+                for g in range(H):
+                    second(done, g, y_bank[done % 2][:, g * D : (g + 1) * D], range(NPASS))
+            for piece in second_k_pieces.get(step, ()):
+                cast_second_k(piece)
+            if done >= 1:
+                normalise(done - 1, y_bank[(done - 1) % 2], H)
+            relu_scale(step, 2)
+            square(step, 2)
+            relu_scale(step, 3)
+            square(step, 3)
+            if done >= 0:
+                den_add(done, y_bank[done % 2], H)
+            if step < last:
+                scores(step + 1, (2, 3))
+
+        b = NQB - 1
+        stage = w_stage[last % W_BUFS]
+        second(b, H - 1, y_bank[3][:, 0:D], (0,))
+        quantize(w_mx[last], 0, stage[:, 0 : 2 * BANK])
+        den_rec(b - 1, H)
+        quantize(w_mx[last], 2 * QB, stage[:, 2 * BANK : 3 * BANK])
+        quantize(w_mx[last], 3 * QB, stage[:, 3 * BANK : 4 * BANK])
+        for g in range(H - 1):
+            second(b, g, y_bank[2][:, g * D : (g + 1) * D], range(NPASS))
+        second(b, H - 1, y_bank[3][:, 0:D], (1,))
+        normalise(b - 1, y_bank[(b - 1) % 2], H)
+        den_add(b, y_bank[2], H - 1)
+        den_add(b + 1, y_bank[3], 1)
+        den_rec(b, H - 1)
+        den_rec(b + 1, 1)
+        nc.vector.tensor_scalar(out=o_last[:], in0=y_bank[3][:, 0:D], scalar1=rec[b + 1][:, 0:1], scalar2=None, op0=ALU.mult)
+        normalise(b, y_bank[2], H - 1)
+        nc.sync.dma_start(out=out[H - 1, b * QB : (b + 1) * QB, :], in_=o_last[:])

@@ -26,6 +26,7 @@ STEPS = NPASS * NQB
 X_BUFS = 8
 W_BUFS = 3
 TINY = 2.0 ** -126
+ORDER = [(0, 0), (0, 1), (0, 2), (1, 0), (1, 1), (1, 2), (0, 3), (1, 3)]
 
 
 def tile_rows_relu2_kernel(tc, qT, kT, t, v, out):
@@ -44,10 +45,11 @@ def tile_rows_relu2_kernel(tc, qT, kT, t, v, out):
         q_hbm = qT.rearrange("h (p j) n -> (h p) j n", j=PACK)
         k_hbm = kT.rearrange("h (p j) n -> (h p) j n", j=PACK)
 
-        q_raw = tiles("q_raw", 2, PACK * QB, F32) + tiles("q_raw_rest", 1, PACK * 2 * QB, F32)
+        q_raw = tiles("q_raw", NQB, PACK * QB, F32)
         k_raw = tiles("k_raw", 2 * NPASS, PACK * HALF, F32)
         v_raw = tiles("v_raw", H, NPASS * PACK * D, F32)
-        q_stage = tiles("q_stage", 2, PACK * QB, BF16)
+        q_stage = tiles("q_stage", NQB, PACK * QB, BF16)
+        v_stage = tiles("v_stage", H, NPASS * PACK * D, BF16)
         k_stage0 = tiles("k_stage_first", 4, 2 * HALF, BF16)
         k_stage1 = tiles("k_stage_second", 1, PACK * PASS, BF16)[0]
         w_stage = tiles("w_stage", W_BUFS, H * BANK, BF16)
@@ -85,9 +87,7 @@ def tile_rows_relu2_kernel(tc, qT, kT, t, v, out):
             return flat.rearrange("p (u i j) -> p u j i", i=PACK, j=PACK)
 
         def q_rows(b):
-            if b < 2:
-                return q_raw[b][:].rearrange("p (j n) -> p j n", j=PACK)
-            return q_raw[2][:].rearrange("p (j n) -> p j n", j=PACK)[:, :, (b - 2) * QB : (b - 1) * QB]
+            return q_raw[b][:].rearrange("p (j n) -> p j n", j=PACK)
 
         def k_src(half, pair):
             return k_raw[half][:].rearrange("p (j s r) -> p s j r", j=PACK, r=PACK)[:, :, :, 2 * pair : 2 * pair + 2]
@@ -110,14 +110,14 @@ def tile_rows_relu2_kernel(tc, qT, kT, t, v, out):
             )
 
         def scores(step, heads):
-            c, b = divmod(step, NQB)
+            c, b = ORDER[step]
             for r in range(PACK):
                 for g in heads:
                     rows = slice(ROWS * g, ROWS * (g + 1))
                     mm(score[g][:, r * QB : (r + 1) * QB], k_mx[c], rows, r * P, q_mx[b], rows, 0, True, True)
 
         def relu_scale(step, g):
-            c = step // NQB
+            c = ORDER[step][0]
             nc.vector.scalar_tensor_tensor(
                 out=x_buf[(step * H + g) % X_BUFS][:].rearrange("p (n r) -> p n r", r=PACK),
                 in0=score[g][:].rearrange("p (r n) -> p n r", r=PACK),
@@ -134,22 +134,40 @@ def tile_rows_relu2_kernel(tc, qT, kT, t, v, out):
                 func=ACT.Square,
             )
 
-        def v_stage(g):
-            return w_stage[g % W_BUFS][:, 0 : NPASS * PACK * D]
-
-        def cast_v(g):
-            for c in range(NPASS):
-                cols = slice(c * PACK * D, (c + 1) * PACK * D)
-                nc.gpsimd.tensor_tensor(
-                    out=walk_dst(v_stage(g)[:, cols]),
-                    in0=walk_src(v_raw[g][:, cols].rearrange("p (j e) -> p j e", j=PACK)),
-                    in1=t_sign[:, c * PACK : (c + 1) * PACK].unsqueeze(1).unsqueeze(3).to_broadcast([P, D // PACK, PACK, PACK]),
-                    op=ALU.mult,
+        def relu_scale_square_on_scalar(step, heads):
+            c = ORDER[step][0]
+            for g in heads:
+                for r in range(PACK):
+                    cols = slice(r * QB, (r + 1) * QB)
+                    nc.scalar.activation(
+                        out=x_buf[(step * H + g) % X_BUFS][:, cols],
+                        in_=score[g][:, cols],
+                        func=ACT.Relu,
+                        scale=t_root[:, c * PACK + r : c * PACK + r + 1],
+                    )
+            for g in heads:
+                nc.scalar.activation(
+                    out=walk_dst(w_stage[step % W_BUFS][:, g * BANK : (g + 1) * BANK]),
+                    in_=walk_src(x_buf[(step * H + g) % X_BUFS][:].rearrange("p (r n) -> p r n", r=PACK)),
+                    func=ACT.Square,
                 )
+
+        def cast_v(piece):
+            g, c = divmod(piece, NPASS)
+            cols = slice(c * PACK * D, (c + 1) * PACK * D)
+            nc.vector.tensor_tensor(
+                out=walk_dst(v_stage[g][:, cols]),
+                in0=walk_src(v_raw[g][:, cols].rearrange("p (j e) -> p j e", j=PACK)),
+                in1=t_sign[:, c * PACK : (c + 1) * PACK].unsqueeze(1).unsqueeze(3).to_broadcast([P, D // PACK, PACK, PACK]),
+                op=ALU.mult,
+            )
+
+        def cast_q(b):
+            nc.scalar.copy(out=walk_dst(q_stage[b][:]), in_=walk_src(q_rows(b)))
 
         def second(b, g, dst, passes):
             for c in passes:
-                mm(dst, w_mx[c * NQB + b], slice(0, P), g * QB, v_mx[g], slice(0, P), c * D, c == 0, c == NPASS - 1)
+                mm(dst, w_mx[ORDER.index((c, b))], slice(0, P), g * QB, v_mx[g], slice(0, P), c * D, c == 0, c == NPASS - 1)
 
         def den_add(slot, bank, count):
             nc.vector.tensor_scalar(
@@ -179,18 +197,19 @@ def tile_rows_relu2_kernel(tc, qT, kT, t, v, out):
         load_k(0)
         load_k(1)
         load_q(q_raw[1], QB, QB)
-        load_q(q_raw[2], 2 * QB, 2 * QB)
+        load_q(q_raw[2], 2 * QB, QB)
         load_k(2)
         load_k(3)
         for g in range(H):
             load_v(g)
+        load_q(q_raw[3], 3 * QB, QB)
 
         nc.vector.scalar_tensor_tensor(out=t_abs[:], in0=t_raw[:], scalar=-1.0, in1=t_raw[:], op0=ALU.mult, op1=ALU.max)
         nc.vector.tensor_scalar(out=t_safe[:], in0=t_abs[:], scalar1=TINY, scalar2=None, op0=ALU.max)
         nc.scalar.activation(out=r0[:], in_=t_safe[:], func=ACT.Abs_reciprocal_sqrt)
         nc.gpsimd.tensor_scalar(out=t_pos[:], in0=t_raw[:], scalar1=0.0, scalar2=2.0, op0=ALU.is_ge, op1=ALU.mult)
         nc.gpsimd.tensor_scalar(out=t_sign[:], in0=t_pos[:], scalar1=1.0, scalar2=-1.0, op0=ALU.mult, op1=ALU.add)
-        nc.scalar.copy(out=walk_dst(q_stage[0][:]), in_=walk_src(q_rows(0)))
+        cast_q(0)
         nc.vector.tensor_tensor(out=s0[:], in0=t_abs[:], in1=r0[:], op=ALU.mult)
 
         def first_k_dst(half, pair):
@@ -213,7 +232,7 @@ def tile_rows_relu2_kernel(tc, qT, kT, t, v, out):
         first_k_quantize(1, 1)
         scores(0, (0, 1))
         scores(0, (2, 3))
-        nc.scalar.copy(out=walk_dst(q_stage[1][:]), in_=walk_src(q_rows(1)))
+        cast_q(1)
 
         def cast_second_k(piece):
             half, pair = divmod(piece, 2)
@@ -222,44 +241,49 @@ def tile_rows_relu2_kernel(tc, qT, kT, t, v, out):
                 out=dst[:, half * (P // 2) : (half + 1) * (P // 2), :, 2 * pair : 2 * pair + 2], in_=k_src(2 + half, pair)
             )
 
-        second_k_pieces = {0: (0,), 1: (1, 2), 2: (3,)}
+        second_k_pieces = {0: (0,), 1: (1, 2, 3)}
+        q_cast_at = {0: 2, 4: 3}
+        q_quantize_at = {0: 1, 1: 2, 5: 3}
+        v_cast_at = {1: (0, 1, 2), 2: (3, 4, 5), 3: (6, 7)}
+        v_quantize_at = {2: (0,), 3: (1, 2), 4: (3,)}
+        on_scalar = {2: (2, 3), 3: (3,)}
+        first_y = 4
         last = STEPS - 1
         for step in range(STEPS):
+            done = step - first_y
             for g in (0, 1):
                 relu_scale(step, g)
                 square(step, g)
-                if g == 0 and step - 2 - NQB >= 0:
-                    den_rec(step - 2 - NQB, H)
-            if step + 1 < NQB:
-                quantize(q_mx[step + 1], 0, q_stage[1 if step < 2 else 0][:])
-            if step + 1 == NQB:
+                if g == 0 and done >= 1:
+                    den_rec(done - 1, H)
+            if step in q_quantize_at:
+                quantize(q_mx[q_quantize_at[step]], 0, q_stage[q_quantize_at[step]][:])
+            if step == 2:
                 quantize(k_mx[1], 0, k_stage1[:])
             if step < last:
                 scores(step + 1, (0, 1))
-            if 2 <= step < 2 + H:
-                quantize(v_mx[step - 2], 0, v_stage(step - 2))
+            for g in v_quantize_at.get(step, ()):
+                quantize(v_mx[g], 0, v_stage[g][:])
+            for piece in v_cast_at.get(step, ()):
+                cast_v(piece)
             if step >= 1:
                 quantize(w_mx[step - 1], 0, w_stage[(step - 1) % W_BUFS][:])
-            if step == 0:
-                for b in (2, 3):
-                    nc.gpsimd.tensor_scalar(
-                        out=walk_dst(q_stage[3 - b][:]), in0=walk_src(q_rows(b)), scalar1=1.0, scalar2=0.0, op0=ALU.mult, op1=ALU.add
-                    )
-            if 1 <= step < 1 + H:
-                cast_v(step - 1)
-            done = step - 1 - NQB
-            if done >= 0:
+            if 0 <= done < NQB - 1:
                 for g in range(H):
                     second(done, g, y_bank[done % 2][:, g * D : (g + 1) * D], range(NPASS))
+            if step in q_cast_at:
+                cast_q(q_cast_at[step])
             for piece in second_k_pieces.get(step, ()):
                 cast_second_k(piece)
             if done >= 1:
                 normalise(done - 1, y_bank[(done - 1) % 2], H)
-            relu_scale(step, 2)
-            square(step, 2)
-            relu_scale(step, 3)
-            square(step, 3)
-            if done >= 0:
+            moved = on_scalar.get(step, ())
+            relu_scale_square_on_scalar(step, moved)
+            for g in (2, 3):
+                if g not in moved:
+                    relu_scale(step, g)
+                    square(step, g)
+            if 0 <= done < NQB - 1:
                 den_add(done, y_bank[done % 2], H)
             if step < last:
                 scores(step + 1, (2, 3))
@@ -268,13 +292,11 @@ def tile_rows_relu2_kernel(tc, qT, kT, t, v, out):
         stage = w_stage[last % W_BUFS]
         second(b, H - 1, y_bank[3][:, 0:D], (0,))
         quantize(w_mx[last], 0, stage[:, 0 : 2 * BANK])
-        den_rec(b - 1, H)
         quantize(w_mx[last], 2 * QB, stage[:, 2 * BANK : 3 * BANK])
-        quantize(w_mx[last], 3 * QB, stage[:, 3 * BANK : 4 * BANK])
         for g in range(H - 1):
             second(b, g, y_bank[2][:, g * D : (g + 1) * D], range(NPASS))
+        quantize(w_mx[last], 3 * QB, stage[:, 3 * BANK : 4 * BANK])
         second(b, H - 1, y_bank[3][:, 0:D], (1,))
-        normalise(b - 1, y_bank[(b - 1) % 2], H)
         den_add(b, y_bank[2], H - 1)
         den_add(b + 1, y_bank[3], 1)
         den_rec(b, H - 1)

@@ -23,8 +23,7 @@ NPASS = N // PASS
 HALF = PASS // 2
 BANK = 512
 STEPS = NPASS * NQB
-X_BUFS = 8
-W_BUFS = 3
+X_BUFS = STEPS
 TINY = 2.0 ** -126
 ORDER = [(0, 0), (0, 1), (0, 2), (1, 0), (1, 1), (1, 2), (0, 3), (1, 3)]
 
@@ -45,24 +44,24 @@ def tile_rows_relu2_kernel(tc, qT, kT, t, v, out):
         q_hbm = qT.rearrange("h (p j) n -> (h p) j n", j=PACK)
         k_hbm = kT.rearrange("h (p j) n -> (h p) j n", j=PACK)
 
-        q_raw = tiles("q_raw", NQB, PACK * QB, F32)
+        q_raw = tiles("q_raw", 2, PACK * QB, F32) + tiles("q_raw_rest", 1, PACK * 2 * QB, F32)
         k_raw = tiles("k_raw", 2 * NPASS, PACK * HALF, F32)
         v_raw = tiles("v_raw", H, NPASS * PACK * D, F32)
         q_stage = tiles("q_stage", NQB, PACK * QB, BF16)
-        v_stage = tiles("v_stage", H, NPASS * PACK * D, BF16)
+        v_stage = tiles("v_stage", 2, NPASS * PACK * D, BF16)
         k_stage0 = tiles("k_stage_first", 4, 2 * HALF, BF16)
         k_stage1 = tiles("k_stage_second", 1, PACK * PASS, BF16)[0]
-        w_stage = tiles("w_stage", W_BUFS, H * BANK, BF16)
-        x_buf = tiles("x_buf", X_BUFS, BANK, F32)
+        w_stage = tiles("w_stage", STEPS, H * BANK, BF16)
+        x_buf = tiles("x_buf", X_BUFS, H * BANK, F32)
+        x_rows = tiles("x_rows", 2, BANK, F32)
         q_mx = planes("q", NQB, QB)
         k_mx = planes("k", NPASS, PASS)
         v_mx = planes("v", H, NPASS * D)
         w_mx = planes("w", STEPS, H * QB)
         t_raw, t_abs, t_safe, r0, s0, corr, t_root, t_pos, t_sign = tiles("t_col", 9, NPASS * PACK, F32)
-        den = tiles("den", NQB + 1, H, F32)
-        rec = tiles("rec", NQB + 1, H, F32)
-        o_buf = tiles("o_buf", NQB, H * D, F32)
-        o_last = tiles("o_last", 1, D, F32)[0]
+        den = tiles("den", NQB + 2, H, F32)
+        rec = tiles("rec", NQB + 2, H, F32)
+        o_buf = tiles("o_buf", NQB + 2, H * D, F32)
         score = [ps.tile([P, BANK], F32, name="score%d" % g) for g in range(H)]
         y_bank = [ps.tile([P, BANK], F32, name="y%d" % b) for b in range(4)]
 
@@ -87,7 +86,9 @@ def tile_rows_relu2_kernel(tc, qT, kT, t, v, out):
             return flat.rearrange("p (u i j) -> p u j i", i=PACK, j=PACK)
 
         def q_rows(b):
-            return q_raw[b][:].rearrange("p (j n) -> p j n", j=PACK)
+            if b < 2:
+                return q_raw[b][:].rearrange("p (j n) -> p j n", j=PACK)
+            return q_raw[2][:].rearrange("p (j n) -> p j n", j=PACK)[:, :, (b - 2) * QB : (b - 1) * QB]
 
         def k_src(half, pair):
             return k_raw[half][:].rearrange("p (j s r) -> p s j r", j=PACK, r=PACK)[:, :, :, 2 * pair : 2 * pair + 2]
@@ -109,56 +110,69 @@ def tile_rows_relu2_kernel(tc, qT, kT, t, v, out):
                 stop=stop,
             )
 
-        def scores(step, heads):
+        def scores(step, g):
             c, b = ORDER[step]
+            rows = slice(ROWS * g, ROWS * (g + 1))
             for r in range(PACK):
-                for g in heads:
-                    rows = slice(ROWS * g, ROWS * (g + 1))
-                    mm(score[g][:, r * QB : (r + 1) * QB], k_mx[c], rows, r * P, q_mx[b], rows, 0, True, True)
+                mm(score[g][:, r * QB : (r + 1) * QB], k_mx[c], rows, r * P, q_mx[b], rows, 0, True, True)
 
-        def relu_scale(step, g):
+        def relu_scale(step, g, first=0, count=QB):
             c = ORDER[step][0]
+            col = g * BANK + first * PACK
             nc.vector.scalar_tensor_tensor(
-                out=x_buf[(step * H + g) % X_BUFS][:].rearrange("p (n r) -> p n r", r=PACK),
-                in0=score[g][:].rearrange("p (r n) -> p n r", r=PACK),
+                out=x_buf[step % X_BUFS][:, col : col + count * PACK].rearrange("p (n r) -> p n r", r=PACK),
+                in0=score[g][:].rearrange("p (r n) -> p n r", r=PACK)[:, first : first + count, :],
                 scalar=0.0,
-                in1=t_root[:, c * PACK : (c + 1) * PACK].unsqueeze(1).to_broadcast([P, QB, PACK]),
+                in1=t_root[:, c * PACK : (c + 1) * PACK].unsqueeze(1).to_broadcast([P, count, PACK]),
                 op0=ALU.max,
                 op1=ALU.mult,
             )
 
-        def square(step, g):
+        def square(step, first, width):
+            cols = slice(first, first + width)
+            nc.scalar.activation(out=w_stage[step][:, cols], in_=x_buf[step % X_BUFS][:, cols], func=ACT.Square)
+
+        def square_on_gpsimd(step):
+            x = x_buf[step % X_BUFS][:, 0:BANK]
+            nc.gpsimd.tensor_tensor(out=q_stage[1][:], in0=x, in1=x, op=ALU.mult)
+
+        def quantize_w(step, first, count):
+            quantize(w_mx[step], first * QB, w_stage[step][:, first * BANK : (first + count) * BANK])
+
+        def relu_scale_on_scalar(step, g):
+            c = ORDER[step][0]
+            for r in range(PACK):
+                cols = slice(r * QB, (r + 1) * QB)
+                nc.scalar.activation(
+                    out=x_rows[step % 2][:, cols],
+                    in_=score[g][:, cols],
+                    func=ACT.Relu,
+                    scale=t_root[:, c * PACK + r : c * PACK + r + 1],
+                )
+
+        def square_rows(step, g):
             nc.scalar.activation(
-                out=w_stage[step % W_BUFS][:, g * BANK : (g + 1) * BANK],
-                in_=x_buf[(step * H + g) % X_BUFS][:],
+                out=walk_dst(w_stage[step][:, g * BANK : (g + 1) * BANK]),
+                in_=walk_src(x_rows[step % 2][:].rearrange("p (r n) -> p r n", r=PACK)),
                 func=ACT.Square,
             )
 
-        def relu_scale_square_on_scalar(step, heads):
-            c = ORDER[step][0]
-            for g in heads:
-                for r in range(PACK):
-                    cols = slice(r * QB, (r + 1) * QB)
-                    nc.scalar.activation(
-                        out=x_buf[(step * H + g) % X_BUFS][:, cols],
-                        in_=score[g][:, cols],
-                        func=ACT.Relu,
-                        scale=t_root[:, c * PACK + r : c * PACK + r + 1],
-                    )
-            for g in heads:
-                nc.scalar.activation(
-                    out=walk_dst(w_stage[step % W_BUFS][:, g * BANK : (g + 1) * BANK]),
-                    in_=walk_src(x_buf[(step * H + g) % X_BUFS][:].rearrange("p (r n) -> p r n", r=PACK)),
-                    func=ACT.Square,
-                )
+        def v_rows(g, c):
+            return v_raw[g][:, c * PACK * D : (c + 1) * PACK * D].rearrange("p (j e) -> p j e", j=PACK)
 
-        def cast_v(piece):
-            g, c = divmod(piece, NPASS)
-            cols = slice(c * PACK * D, (c + 1) * PACK * D)
+        def cast_v(g, c):
             nc.vector.tensor_tensor(
-                out=walk_dst(v_stage[g][:, cols]),
-                in0=walk_src(v_raw[g][:, cols].rearrange("p (j e) -> p j e", j=PACK)),
+                out=walk_dst(v_stage[g - 2][:, c * PACK * D : (c + 1) * PACK * D]),
+                in0=walk_src(v_rows(g, c)),
                 in1=t_sign[:, c * PACK : (c + 1) * PACK].unsqueeze(1).unsqueeze(3).to_broadcast([P, D // PACK, PACK, PACK]),
+                op=ALU.mult,
+            )
+
+        def cast_v_on_gpsimd(g, c):
+            nc.gpsimd.tensor_tensor(
+                out=q_stage[1][:].rearrange("p (e j) -> p e j", j=PACK),
+                in0=v_rows(g, c).rearrange("p j e -> p e j"),
+                in1=t_sign[:, c * PACK : (c + 1) * PACK].unsqueeze(1).to_broadcast([P, D, PACK]),
                 op=ALU.mult,
             )
 
@@ -181,13 +195,23 @@ def tile_rows_relu2_kernel(tc, qT, kT, t, v, out):
         def den_rec(slot, count):
             nc.vector.reciprocal(out=rec[slot][:, 0:count], in_=den[slot][:, 0:count])
 
-        def normalise(b, bank, count):
+        def store(slot, b, heads, count):
+            nc.sync.dma_start(
+                out=out[heads, b * QB : (b + 1) * QB, :].rearrange("g m e -> m g e"),
+                in_=o_buf[slot][:, 0 : count * D].rearrange("p (g e) -> p g e", e=D),
+            )
+
+        def normalise(slot, bank, count):
             for g in range(count):
                 cols = slice(g * D, (g + 1) * D)
-                nc.scalar.activation(out=o_buf[b][:, cols], in_=bank[:, cols], func=ACT.Copy, scale=rec[b][:, g : g + 1])
-            nc.sync.dma_start(
-                out=out[0:count, b * QB : (b + 1) * QB, :].rearrange("g m e -> m g e"),
-                in_=o_buf[b][:, 0 : count * D].rearrange("p (g e) -> p g e", e=D),
+                nc.scalar.activation(out=o_buf[slot][:, cols], in_=bank[:, cols], func=ACT.Copy, scale=rec[slot][:, g : g + 1])
+
+        def normalise_on_vector(slot, bank, count):
+            nc.vector.tensor_tensor(
+                out=o_buf[slot][:, 0 : count * D].rearrange("p (g e) -> p g e", e=D),
+                in0=bank[:, 0 : count * D].rearrange("p (g e) -> p g e", e=D),
+                in1=rec[slot][:, 0:count].unsqueeze(2).to_broadcast([P, count, D]),
+                op=ALU.mult,
             )
 
         nc.scalar.dma_start(
@@ -197,12 +221,13 @@ def tile_rows_relu2_kernel(tc, qT, kT, t, v, out):
         load_k(0)
         load_k(1)
         load_q(q_raw[1], QB, QB)
-        load_q(q_raw[2], 2 * QB, QB)
+        load_q(q_raw[2], 2 * QB, 2 * QB)
+        load_v(0)
         load_k(2)
         load_k(3)
-        for g in range(H):
-            load_v(g)
-        load_q(q_raw[3], 3 * QB, QB)
+        load_v(2)
+        load_v(1)
+        load_v(3)
 
         nc.vector.scalar_tensor_tensor(out=t_abs[:], in0=t_raw[:], scalar=-1.0, in1=t_raw[:], op0=ALU.mult, op1=ALU.max)
         nc.vector.tensor_scalar(out=t_safe[:], in0=t_abs[:], scalar1=TINY, scalar2=None, op0=ALU.max)
@@ -230,9 +255,12 @@ def tile_rows_relu2_kernel(tc, qT, kT, t, v, out):
         nc.scalar.copy(out=first_k_dst(1, 1), in_=k_src(1, 1))
         first_k_quantize(1, 0)
         first_k_quantize(1, 1)
-        scores(0, (0, 1))
-        scores(0, (2, 3))
+        for g in range(H):
+            scores(0, g)
         cast_q(1)
+        cast_q(2)
+        cast_q(3)
+        quantize(q_mx[1], 0, q_stage[1][:])
 
         def cast_second_k(piece):
             half, pair = divmod(piece, 2)
@@ -241,66 +269,109 @@ def tile_rows_relu2_kernel(tc, qT, kT, t, v, out):
                 out=dst[:, half * (P // 2) : (half + 1) * (P // 2), :, 2 * pair : 2 * pair + 2], in_=k_src(2 + half, pair)
             )
 
-        second_k_pieces = {0: (0,), 1: (1, 2, 3)}
-        q_cast_at = {0: 2, 4: 3}
-        q_quantize_at = {0: 1, 1: 2, 5: 3}
-        v_cast_at = {1: (0, 1, 2), 2: (3, 4, 5), 3: (6, 7)}
-        v_quantize_at = {2: (0,), 3: (1, 2), 4: (3,)}
-        on_scalar = {2: (2, 3), 3: (3,)}
+        q_quantize_at = {1: 2, 5: 3}
+        scalar_reads = (2, 3, 4, 5, 6, 7)
         first_y = 4
         last = STEPS - 1
         for step in range(STEPS):
             done = step - first_y
-            for g in (0, 1):
-                relu_scale(step, g)
-                square(step, g)
-                if g == 0 and done >= 1:
-                    den_rec(done - 1, H)
+            relu_scale(step, 0)
+            if step in scalar_reads:
+                relu_scale_on_scalar(step, 2)
+                if step < first_y:
+                    square(step, 0, BANK)
+                else:
+                    if 2 <= done:
+                        normalise(done - 2, y_bank[done % 2], H)
+                        store(done - 2, done - 2, slice(0, H), H)
+                if step in (4, 5):
+                    square(2, (2 * step - 7) * BANK, BANK)
+                square_rows(step, 2)
             if step in q_quantize_at:
                 quantize(q_mx[q_quantize_at[step]], 0, q_stage[q_quantize_at[step]][:])
+            if step < last and step != 2:
+                scores(step + 1, 0)
+            if step in (3, 4):
+                quantize(v_mx[step - 1], 0, v_stage[step - 3][:])
+            if step in (2, 3):
+                for c in range(NPASS):
+                    cast_v(step, c)
             if step == 2:
                 quantize(k_mx[1], 0, k_stage1[:])
-            if step < last:
-                scores(step + 1, (0, 1))
-            for g in v_quantize_at.get(step, ()):
-                quantize(v_mx[g], 0, v_stage[g][:])
-            for piece in v_cast_at.get(step, ()):
-                cast_v(piece)
-            if step >= 1:
-                quantize(w_mx[step - 1], 0, w_stage[(step - 1) % W_BUFS][:])
+                scores(step + 1, 0)
+            if 0 <= done < NQB - 1:
+                quantize_w(done, 0, H)
+            if done >= 1:
+                den_add(done - 1, y_bank[(done - 1) % 2], H)
+            if done == 0:
+                quantize_w(step - 1, 0, H)
+            if done >= 1:
+                quantize_w(step - 1, 1, 1)
+                quantize_w(step - 1, 2, 2)
+                den_rec(done - 1, H)
+                quantize(w_mx[step - 1], 0, q_stage[1][:])
+            if 1 <= step <= H:
+                quantize(v_mx[(step - 1) // 2], (step - 1) % 2 * D, q_stage[1][:])
+            if step < H:
+                cast_v_on_gpsimd(step // 2, step % 2)
+            else:
+                square_on_gpsimd(step)
+            if step in scalar_reads and step < last:
+                scores(step + 1, 2)
             if 0 <= done < NQB - 1:
                 for g in range(H):
                     second(done, g, y_bank[done % 2][:, g * D : (g + 1) * D], range(NPASS))
-            if step in q_cast_at:
-                cast_q(q_cast_at[step])
-            for piece in second_k_pieces.get(step, ()):
-                cast_second_k(piece)
-            if done >= 1:
-                normalise(done - 1, y_bank[(done - 1) % 2], H)
-            moved = on_scalar.get(step, ())
-            relu_scale_square_on_scalar(step, moved)
-            for g in (2, 3):
-                if g not in moved:
-                    relu_scale(step, g)
-                    square(step, g)
-            if 0 <= done < NQB - 1:
-                den_add(done, y_bank[done % 2], H)
+            relu_scale(step, 1)
+            if step == 1:
+                for piece in (1, 2, 3):
+                    cast_second_k(piece)
+            if step == 2:
+                pass
+            elif step in scalar_reads:
+                square(step, BANK, BANK)
+            else:
+                square(step, 0, 2 * BANK)
             if step < last:
-                scores(step + 1, (2, 3))
+                scores(step + 1, 1)
+            if step not in scalar_reads:
+                relu_scale(step, 2)
+                scores(step + 1, 2)
+            if step == 0:
+                cast_second_k(0)
+            if step < last:
+                relu_scale(step, 3)
+                if step == 2:
+                    pass
+                elif step in scalar_reads:
+                    square(step, 3 * BANK, BANK)
+                else:
+                    square(step, 2 * BANK, 2 * BANK)
+                scores(step + 1, 3)
 
         b = NQB - 1
-        stage = w_stage[last % W_BUFS]
-        second(b, H - 1, y_bank[3][:, 0:D], (0,))
-        quantize(w_mx[last], 0, stage[:, 0 : 2 * BANK])
-        quantize(w_mx[last], 2 * QB, stage[:, 2 * BANK : 3 * BANK])
-        for g in range(H - 1):
-            second(b, g, y_bank[2][:, g * D : (g + 1) * D], range(NPASS))
-        quantize(w_mx[last], 3 * QB, stage[:, 3 * BANK : 4 * BANK])
-        second(b, H - 1, y_bank[3][:, 0:D], (1,))
-        den_add(b, y_bank[2], H - 1)
-        den_add(b + 1, y_bank[3], 1)
-        den_rec(b, H - 1)
+        for first in (0, QB // 2):
+            relu_scale(last, H - 1, first, QB // 2)
+            square(last, (H - 1) * BANK + first * PACK, BANK // 2)
+        second(b, 3, y_bank[3][:, 0:D], (0,))
+        normalise_on_vector(b - 1, y_bank[(b - 1) % 2], H)
+        store(b - 1, b - 1, slice(0, H), H)
+        quantize_w(last, 2, 1)
+        quantize(w_mx[last], 0, q_stage[1][:])
+        quantize_w(last, 1, 1)
+        second(b, 2, y_bank[2][:, D : 2 * D], range(NPASS))
+        second(b, 0, y_bank[2][:, 0:D], range(NPASS))
+        second(b, 1, y_bank[1][:, 0:D], range(NPASS))
+        quantize_w(last, 3, 1)
+        second(b, 3, y_bank[3][:, 0:D], (1,))
+        den_add(b, y_bank[2], 2)
+        den_add(b + 1, y_bank[1], 1)
+        den_rec(b, 2)
         den_rec(b + 1, 1)
-        nc.vector.tensor_scalar(out=o_last[:], in0=y_bank[3][:, 0:D], scalar1=rec[b + 1][:, 0:1], scalar2=None, op0=ALU.mult)
-        normalise(b, y_bank[2], H - 1)
-        nc.sync.dma_start(out=out[H - 1, b * QB : (b + 1) * QB, :], in_=o_last[:])
+        den_add(b + 2, y_bank[3], 1)
+        normalise(b, y_bank[2], 2)
+        store(b, b, slice(0, H, 2), 2)
+        den_rec(b + 2, 1)
+        normalise(b + 1, y_bank[1], 1)
+        store(b + 1, b, slice(1, 2), 1)
+        normalise_on_vector(b + 2, y_bank[3], 1)
+        store(b + 2, b, slice(3, 4), 1)

@@ -9,369 +9,379 @@ F32 = mybir.dt.float32
 BF16 = mybir.dt.bfloat16
 U32 = mybir.dt.uint32
 U8 = mybir.dt.uint8
-X4 = mybir.dt.float8_e4m3fn_x4
+FP8X4 = mybir.dt.float8_e4m3fn_x4
 ALU = mybir.AluOpType
 ACT = mybir.ActivationFunctionType
 
 P = 128
 PACK = 4
-ROWS = 32
+ROWS = D // PACK
 QB = 128
-NQB = NQ // QB
+BLOCKS = NQ // QB
 PASS = P * PACK
-NPASS = N // PASS
+PASSES = N // PASS
 HALF = PASS // 2
-BANK = 512
-STEPS = NPASS * NQB
-X_BUFS = STEPS
-TINY = 2.0 ** -126
+BANK = PACK * QB
+SMALLEST = 2.0**-126
+
 ORDER = [(0, 0), (0, 1), (0, 2), (1, 0), (1, 1), (1, 2), (0, 3), (1, 3)]
+STEPS = PASSES * BLOCKS
+LAST = STEPS - 1
+SECOND_KEYS = 2
+FIRST_PRODUCT = 4
+SCALAR_READS_FROM = 2
+SCALAR_HEAD = 2
+PUT_OFF_STEP = 2
+PUT_OFF = {4: 1, 5: 3}
 
 
 def tile_rows_relu2_kernel(tc, qT, kT, t, v, out):
     nc = tc.nc
     with ExitStack() as ctx:
-        sb = ctx.enter_context(tc.tile_pool(name="sb", bufs=1))
-        ps = ctx.enter_context(tc.psum_pool(name="ps", bufs=1))
+        sbuf = ctx.enter_context(tc.tile_pool(name="sbuf", bufs=1))
+        psum = ctx.enter_context(tc.psum_pool(name="psum", bufs=1))
         ctx.enter_context(tc.manual_schedule())
 
-        def tiles(name, count, width, dtype):
-            return [sb.tile([P, width], dtype, name="%s%d" % (name, i), align_bytes=64) for i in range(count)]
+        def tiles(name, widths, dtype):
+            return [sbuf.tile([P, w], dtype, name="%s%d" % (name, i), align_bytes=64) for i, w in enumerate(widths)]
 
-        def planes(name, count, words):
-            return list(zip(tiles(name + "_codes", count, words, U32), tiles(name + "_scales", count, words, U8)))
+        def quantised(name, widths):
+            return list(zip(tiles(name + "_words", widths, U32), tiles(name + "_scales", widths, U8)))
 
-        q_hbm = qT.rearrange("h (p j) n -> (h p) j n", j=PACK)
-        k_hbm = kT.rearrange("h (p j) n -> (h p) j n", j=PACK)
+        q_widths = [QB, QB, 2 * QB]
+        q_raw = tiles("q_raw", [PACK * w for w in q_widths], F32)
+        k_raw = tiles("k_raw", [PACK * HALF] * (N // HALF), F32)
+        v_raw = tiles("v_raw", [PASSES * PACK * D] * H, F32)
+        w_own = tiles("w_stage", [H * BANK] * (FIRST_PRODUCT + 1), BF16)
+        w_stage = w_own + [w_own[FIRST_PRODUCT]] * (LAST - FIRST_PRODUCT - 1) + [w_own[FIRST_PRODUCT - 1]]
+        handover = w_own[FIRST_PRODUCT][:, 0:BANK]
+        q_first, q_rest = tiles("q_stage", [PACK * QB, PACK * 2 * QB], BF16)
+        q_stage = [q_first[:], handover, q_rest[:]]
+        k_first = tiles("k_first", [2 * HALF] * 4, BF16)
+        k_second = tiles("k_second", [PACK * PASS], BF16)[0]
+        v_stage = tiles("v_stage", [PASSES * PACK * D] * 2, BF16)
+        x_words = tiles("x_words", [H * BANK] * STEPS, F32)
+        x_places = tiles("x_places", [BANK] * 2, F32)
+        q_mx = quantised("q", q_widths)
+        k_mx = quantised("k", [PASS] * PASSES)
+        v_mx = quantised("v", [PASSES * D] * H)
+        w_mx = quantised("w", [H * QB] * STEPS)
+        t_raw, t_abs, t_safe, inv_root, root, newton, t_root, t_step, t_sign = tiles("t", [PASSES * PACK] * 9, F32)
+        groups = BLOCKS + 2
+        den = tiles("den", [H] * groups, F32)
+        inv_den = tiles("inv_den", [H] * groups, F32)
+        result = tiles("result", [H * D] * groups, F32)
+        score = [psum.tile([P, BANK], F32, name="score%d" % g) for g in range(H)]
+        y_bank = [psum.tile([P, BANK], F32, name="y%d" % i) for i in range(4)]
 
-        q_raw = tiles("q_raw", 2, PACK * QB, F32) + tiles("q_raw_rest", 1, PACK * 2 * QB, F32)
-        k_raw = tiles("k_raw", 2 * NPASS, PACK * HALF, F32)
-        v_raw = tiles("v_raw", H, NPASS * PACK * D, F32)
-        q_stage = tiles("q_stage", NQB, PACK * QB, BF16)
-        v_stage = tiles("v_stage", 2, NPASS * PACK * D, BF16)
-        k_stage0 = tiles("k_stage_first", 4, 2 * HALF, BF16)
-        k_stage1 = tiles("k_stage_second", 1, PACK * PASS, BF16)[0]
-        w_stage = tiles("w_stage", STEPS, H * BANK, BF16)
-        x_buf = tiles("x_buf", X_BUFS, H * BANK, F32)
-        x_rows = tiles("x_rows", 2, BANK, F32)
-        q_mx = planes("q", NQB, QB)
-        k_mx = planes("k", NPASS, PASS)
-        v_mx = planes("v", H, NPASS * D)
-        w_mx = planes("w", STEPS, H * QB)
-        t_raw, t_abs, t_safe, r0, s0, corr, t_root, t_pos, t_sign = tiles("t_col", 9, NPASS * PACK, F32)
-        den = tiles("den", NQB + 2, H, F32)
-        rec = tiles("rec", NQB + 2, H, F32)
-        o_buf = tiles("o_buf", NQB + 2, H * D, F32)
-        score = [ps.tile([P, BANK], F32, name="score%d" % g) for g in range(H)]
-        y_bank = [ps.tile([P, BANK], F32, name="y%d" % b) for b in range(4)]
+        def rows_of(flat):
+            return flat.rearrange("p (j n) -> p j n", j=PACK)
 
-        def load_q(tile, first, width):
-            nc.sync.dma_start(out=tile[:].rearrange("p (j n) -> p j n", j=PACK), in_=q_hbm[:, :, first : first + width])
+        def walk_rows(rows):
+            return rows.rearrange("p j (u i) -> p u j i", i=PACK)
+
+        def walk_words(flat):
+            return flat.rearrange("p (u i j) -> p u j i", i=PACK, j=PACK)
+
+        def token_values(column_tile, c):
+            return column_tile[:, c * PACK : (c + 1) * PACK]
+
+        def load_q(piece):
+            first = sum(q_widths[:piece])
+            source = qT.rearrange("h (p j) n -> (h p) j n", j=PACK)[:, :, first : first + q_widths[piece]]
+            nc.sync.dma_start(out=rows_of(q_raw[piece][:]), in_=source)
 
         def load_k(half):
-            nc.sync.dma_start(
-                out=k_raw[half][:].rearrange("p (j n) -> p j n", j=PACK), in_=k_hbm[:, :, half * HALF : (half + 1) * HALF]
-            )
+            source = kT.rearrange("h (p j) n -> (h p) j n", j=PACK)[:, :, half * HALF : (half + 1) * HALF]
+            nc.sync.dma_start(out=rows_of(k_raw[half][:]), in_=source)
 
         def load_v(g):
             nc.sync.dma_start(
-                out=v_raw[g][:].rearrange("p (c x) -> p c x", c=NPASS),
-                in_=v[g].rearrange("(c p j) e -> p c (j e)", c=NPASS, j=PACK),
+                out=v_raw[g][:].rearrange("p (c x) -> p c x", c=PASSES),
+                in_=v[g].rearrange("(c p j) e -> p c (j e)", c=PASSES, j=PACK),
             )
 
-        def walk_src(rows):
-            return rows.rearrange("p j (u i) -> p u j i", i=PACK)
+        def cast_q(piece):
+            nc.scalar.copy(out=walk_words(q_stage[piece]), in_=walk_rows(rows_of(q_raw[piece][:])))
 
-        def walk_dst(flat):
-            return flat.rearrange("p (u i j) -> p u j i", i=PACK, j=PACK)
-
-        def q_rows(b):
-            if b < 2:
-                return q_raw[b][:].rearrange("p (j n) -> p j n", j=PACK)
-            return q_raw[2][:].rearrange("p (j n) -> p j n", j=PACK)[:, :, (b - 2) * QB : (b - 1) * QB]
-
-        def k_src(half, pair):
+        def k_tokens(half, pair):
             return k_raw[half][:].rearrange("p (j s r) -> p s j r", j=PACK, r=PACK)[:, :, :, 2 * pair : 2 * pair + 2]
 
-        def quantize(mx, first, stage):
-            words = stage.shape[1] // PACK
-            nc.vector.quantize_mx(
-                out=mx[0][:, first : first + words].bitcast(X4), scales=mx[1][:, first : first + words], in_=stage
+        def cast_first_keys(half):
+            dealt = [k_first[2 * half + pair][:].rearrange("p (r s j) -> p s j r", r=2, j=PACK) for pair in range(2)]
+            nc.vector.tensor_copy(out=dealt[0], in_=k_tokens(half, 0))
+            nc.scalar.copy(out=dealt[1], in_=k_tokens(half, 1))
+
+        def quantise_first_keys(half):
+            for r in range(PACK):
+                stage = k_first[2 * half + r // 2][:, (r % 2) * HALF : (r % 2 + 1) * HALF]
+                quantise(k_mx[0], r * P + half * (P // 2), stage)
+
+        def cast_second_keys(half, pair):
+            dealt = k_second[:].rearrange("p (r s j) -> p s j r", r=PACK, j=PACK)
+            columns = slice(half * (P // 2), (half + 1) * (P // 2))
+            nc.scalar.copy(out=dealt[:, columns, :, 2 * pair : 2 * pair + 2], in_=k_tokens(PASS // HALF + half, pair))
+
+        def v_rows(g, c):
+            return rows_of(v_raw[g][:, c * PACK * D : (c + 1) * PACK * D])
+
+        def cast_v_on_vector(g, c):
+            nc.vector.tensor_tensor(
+                out=walk_words(v_stage[g - 2][:, c * PACK * D : (c + 1) * PACK * D]),
+                in0=walk_rows(v_rows(g, c)),
+                in1=token_values(t_sign, c).unsqueeze(1).unsqueeze(3).to_broadcast([P, D // PACK, PACK, PACK]),
+                op=ALU.mult,
             )
 
-        def mm(dst, lhs, lrows, lcol, rhs, rrows, rcol, start, stop):
+        def cast_v_on_gpsimd(g, c):
+            nc.gpsimd.tensor_tensor(
+                out=handover.rearrange("p (e j) -> p e j", j=PACK),
+                in0=v_rows(g, c).rearrange("p j e -> p e j"),
+                in1=token_values(t_sign, c).unsqueeze(1).to_broadcast([P, D, PACK]),
+                op=ALU.mult,
+            )
+
+        def quantise(target, first, stage):
+            cols = slice(first, first + stage.shape[1] // PACK)
+            nc.vector.quantize_mx(out=target[0][:, cols].bitcast(FP8X4), scales=target[1][:, cols], in_=stage)
+
+        def quantise_w(step, first_head, heads):
+            quantise(w_mx[step], first_head * QB, w_stage[step][:, first_head * BANK : (first_head + heads) * BANK])
+
+        def matmul(dst, rows, lhs, lhs_first, rhs, rhs_first, start, stop):
+            lhs_cols, rhs_cols = slice(lhs_first, lhs_first + P), slice(rhs_first, rhs_first + P)
             nc.tensor.matmul_mx(
                 out=dst,
-                lhsT=lhs[0][lrows, lcol : lcol + P].bitcast(X4),
-                lhsT_scale=lhs[1][lrows, lcol : lcol + P],
-                rhs=rhs[0][rrows, rcol : rcol + P].bitcast(X4),
-                rhs_scale=rhs[1][rrows, rcol : rcol + P],
+                lhsT=lhs[0][rows, lhs_cols].bitcast(FP8X4),
+                lhsT_scale=lhs[1][rows, lhs_cols],
+                rhs=rhs[0][rows, rhs_cols].bitcast(FP8X4),
+                rhs_scale=rhs[1][rows, rhs_cols],
                 start=start,
                 stop=stop,
             )
 
         def scores(step, g):
             c, b = ORDER[step]
+            piece = min(b, len(q_widths) - 1)
             rows = slice(ROWS * g, ROWS * (g + 1))
             for r in range(PACK):
-                mm(score[g][:, r * QB : (r + 1) * QB], k_mx[c], rows, r * P, q_mx[b], rows, 0, True, True)
+                dst = score[g][:, r * QB : (r + 1) * QB]
+                matmul(dst, rows, k_mx[c], r * P, q_mx[piece], (b - piece) * QB, True, True)
 
-        def relu_scale(step, g, first=0, count=QB):
-            c = ORDER[step][0]
+        def second_product(b, g, bank, slot, passes):
+            for c in passes:
+                dst = bank[:, slot * D : (slot + 1) * D]
+                matmul(dst, slice(0, P), w_mx[ORDER.index((c, b))], g * QB, v_mx[g], c * D, c == 0, c == PASSES - 1)
+
+        def read_scores(step, g, first=0, queries=QB):
             col = g * BANK + first * PACK
             nc.vector.scalar_tensor_tensor(
-                out=x_buf[step % X_BUFS][:, col : col + count * PACK].rearrange("p (n r) -> p n r", r=PACK),
-                in0=score[g][:].rearrange("p (r n) -> p n r", r=PACK)[:, first : first + count, :],
+                out=x_words[step][:, col : col + queries * PACK].rearrange("p (n r) -> p n r", r=PACK),
+                in0=score[g][:].rearrange("p (r n) -> p n r", r=PACK)[:, first : first + queries, :],
                 scalar=0.0,
-                in1=t_root[:, c * PACK : (c + 1) * PACK].unsqueeze(1).to_broadcast([P, count, PACK]),
+                in1=token_values(t_root, ORDER[step][0]).unsqueeze(1).to_broadcast([P, queries, PACK]),
                 op0=ALU.max,
                 op1=ALU.mult,
             )
 
-        def square(step, first, width):
-            cols = slice(first, first + width)
-            nc.scalar.activation(out=w_stage[step][:, cols], in_=x_buf[step % X_BUFS][:, cols], func=ACT.Square)
-
-        def square_on_gpsimd(step):
-            x = x_buf[step % X_BUFS][:, 0:BANK]
-            nc.gpsimd.tensor_tensor(out=q_stage[1][:], in0=x, in1=x, op=ALU.mult)
-
-        def quantize_w(step, first, count):
-            quantize(w_mx[step], first * QB, w_stage[step][:, first * BANK : (first + count) * BANK])
-
-        def relu_scale_on_scalar(step, g):
-            c = ORDER[step][0]
+        def read_scores_on_scalar(step):
             for r in range(PACK):
                 cols = slice(r * QB, (r + 1) * QB)
                 nc.scalar.activation(
-                    out=x_rows[step % 2][:, cols],
-                    in_=score[g][:, cols],
+                    out=x_places[step % 2][:, cols],
+                    in_=score[SCALAR_HEAD][:, cols],
                     func=ACT.Relu,
-                    scale=t_root[:, c * PACK + r : c * PACK + r + 1],
+                    scale=token_values(t_root, ORDER[step][0])[:, r : r + 1],
                 )
 
-        def square_rows(step, g):
+        def square(step, first, width):
+            cols = slice(first, first + width)
+            nc.scalar.activation(out=w_stage[step][:, cols], in_=x_words[step][:, cols], func=ACT.Square)
+
+        def square_places(step):
             nc.scalar.activation(
-                out=walk_dst(w_stage[step][:, g * BANK : (g + 1) * BANK]),
-                in_=walk_src(x_rows[step % 2][:].rearrange("p (r n) -> p r n", r=PACK)),
+                out=walk_words(w_stage[step][:, SCALAR_HEAD * BANK : (SCALAR_HEAD + 1) * BANK]),
+                in_=walk_rows(rows_of(x_places[step % 2][:])),
                 func=ACT.Square,
             )
 
-        def v_rows(g, c):
-            return v_raw[g][:, c * PACK * D : (c + 1) * PACK * D].rearrange("p (j e) -> p j e", j=PACK)
+        def square_by_product(engine, step, first, width):
+            x = x_words[step][:, first : first + width]
+            engine.tensor_tensor(out=w_stage[step][:, first : first + width], in0=x, in1=x, op=ALU.mult)
 
-        def cast_v(g, c):
-            nc.vector.tensor_tensor(
-                out=walk_dst(v_stage[g - 2][:, c * PACK * D : (c + 1) * PACK * D]),
-                in0=walk_src(v_rows(g, c)),
-                in1=t_sign[:, c * PACK : (c + 1) * PACK].unsqueeze(1).unsqueeze(3).to_broadcast([P, D // PACK, PACK, PACK]),
-                op=ALU.mult,
-            )
+        def by_head(flat, count):
+            return flat[:, 0 : count * D].rearrange("p (g e) -> p g e", e=D)
 
-        def cast_v_on_gpsimd(g, c):
-            nc.gpsimd.tensor_tensor(
-                out=q_stage[1][:].rearrange("p (e j) -> p e j", j=PACK),
-                in0=v_rows(g, c).rearrange("p j e -> p e j"),
-                in1=t_sign[:, c * PACK : (c + 1) * PACK].unsqueeze(1).to_broadcast([P, D, PACK]),
-                op=ALU.mult,
-            )
-
-        def cast_q(b):
-            nc.scalar.copy(out=walk_dst(q_stage[b][:]), in_=walk_src(q_rows(b)))
-
-        def second(b, g, dst, passes):
-            for c in passes:
-                mm(dst, w_mx[ORDER.index((c, b))], slice(0, P), g * QB, v_mx[g], slice(0, P), c * D, c == 0, c == NPASS - 1)
-
-        def den_add(slot, bank, count):
+        def denominators(group, bank, count):
             nc.vector.tensor_scalar(
-                out=den[slot][:, 0:count],
-                in0=bank[:].rearrange("p (g e) -> p g e", e=D)[:, 0:count, D - 1],
-                scalar1=1.0,
-                scalar2=None,
-                op0=ALU.add,
+                out=den[group][:, 0:count], in0=by_head(bank, count)[:, :, D - 1], scalar1=1.0, scalar2=None, op0=ALU.add
             )
 
-        def den_rec(slot, count):
-            nc.vector.reciprocal(out=rec[slot][:, 0:count], in_=den[slot][:, 0:count])
+        def invert(group, count):
+            nc.vector.reciprocal(out=inv_den[group][:, 0:count], in_=den[group][:, 0:count])
 
-        def store(slot, b, heads, count):
-            nc.sync.dma_start(
-                out=out[heads, b * QB : (b + 1) * QB, :].rearrange("g m e -> m g e"),
-                in_=o_buf[slot][:, 0 : count * D].rearrange("p (g e) -> p g e", e=D),
-            )
+        def divide_on_scalar(group, bank, count):
+            for i in range(count):
+                cols = slice(i * D, (i + 1) * D)
+                nc.scalar.activation(
+                    out=result[group][:, cols], in_=bank[:, cols], func=ACT.Copy, scale=inv_den[group][:, i : i + 1]
+                )
 
-        def normalise(slot, bank, count):
-            for g in range(count):
-                cols = slice(g * D, (g + 1) * D)
-                nc.scalar.activation(out=o_buf[slot][:, cols], in_=bank[:, cols], func=ACT.Copy, scale=rec[slot][:, g : g + 1])
-
-        def normalise_on_vector(slot, bank, count):
+        def divide_on_vector(group, bank, count):
             nc.vector.tensor_tensor(
-                out=o_buf[slot][:, 0 : count * D].rearrange("p (g e) -> p g e", e=D),
-                in0=bank[:, 0 : count * D].rearrange("p (g e) -> p g e", e=D),
-                in1=rec[slot][:, 0:count].unsqueeze(2).to_broadcast([P, count, D]),
+                out=by_head(result[group], count),
+                in0=by_head(bank, count),
+                in1=inv_den[group][:, 0:count].unsqueeze(2).to_broadcast([P, count, D]),
                 op=ALU.mult,
             )
+
+        def store(group, b, heads, count):
+            target = out[heads, b * QB : (b + 1) * QB, :].rearrange("g m e -> m g e")
+            nc.sync.dma_start(out=target, in_=by_head(result[group], count))
 
         nc.scalar.dma_start(
-            out=t_raw[:].rearrange("p (c j) -> p c j", c=NPASS), in_=t.rearrange("(c p j) o -> p c (j o)", c=NPASS, j=PACK)
+            out=t_raw[:].rearrange("p (c j) -> p c j", c=PASSES), in_=t.rearrange("(c p j) o -> p c (j o)", c=PASSES, j=PACK)
         )
-        load_q(q_raw[0], 0, QB)
+        load_q(0)
         load_k(0)
         load_k(1)
-        load_q(q_raw[1], QB, QB)
-        load_q(q_raw[2], 2 * QB, 2 * QB)
+        load_q(1)
+        load_q(2)
         load_v(0)
         load_k(2)
         load_k(3)
-        load_v(2)
-        load_v(1)
-        load_v(3)
+        for g in (2, 1, 3):
+            load_v(g)
 
+        nc.vector.tensor_copy(out=walk_words(q_stage[0]), in_=walk_rows(rows_of(q_raw[0][:])))
         nc.vector.scalar_tensor_tensor(out=t_abs[:], in0=t_raw[:], scalar=-1.0, in1=t_raw[:], op0=ALU.mult, op1=ALU.max)
-        nc.vector.tensor_scalar(out=t_safe[:], in0=t_abs[:], scalar1=TINY, scalar2=None, op0=ALU.max)
-        nc.scalar.activation(out=r0[:], in_=t_safe[:], func=ACT.Abs_reciprocal_sqrt)
-        nc.gpsimd.tensor_scalar(out=t_pos[:], in0=t_raw[:], scalar1=0.0, scalar2=2.0, op0=ALU.is_ge, op1=ALU.mult)
-        nc.gpsimd.tensor_scalar(out=t_sign[:], in0=t_pos[:], scalar1=1.0, scalar2=-1.0, op0=ALU.mult, op1=ALU.add)
-        cast_q(0)
-        nc.vector.tensor_tensor(out=s0[:], in0=t_abs[:], in1=r0[:], op=ALU.mult)
-
-        def first_k_dst(half, pair):
-            return k_stage0[2 * half + pair][:].rearrange("p (r s j) -> p s j r", r=2, j=PACK)
-
-        def first_k_quantize(half, pair):
-            for rr in range(2):
-                quantize(k_mx[0], (2 * pair + rr) * P + half * (P // 2), k_stage0[2 * half + pair][:, rr * HALF : (rr + 1) * HALF])
-
-        nc.vector.tensor_copy(out=first_k_dst(0, 0), in_=k_src(0, 0))
-        nc.scalar.copy(out=first_k_dst(0, 1), in_=k_src(0, 1))
-        nc.vector.scalar_tensor_tensor(out=corr[:], in0=s0[:], scalar=-0.5, in1=r0[:], op0=ALU.mult, op1=ALU.mult)
-        quantize(q_mx[0], 0, q_stage[0][:])
-        nc.vector.scalar_tensor_tensor(out=t_root[:], in0=corr[:], scalar=1.5, in1=s0[:], op0=ALU.add, op1=ALU.mult)
-        first_k_quantize(0, 0)
-        first_k_quantize(0, 1)
-        nc.vector.tensor_copy(out=first_k_dst(1, 0), in_=k_src(1, 0))
-        nc.scalar.copy(out=first_k_dst(1, 1), in_=k_src(1, 1))
-        first_k_quantize(1, 0)
-        first_k_quantize(1, 1)
+        nc.vector.tensor_scalar(out=t_safe[:], in0=t_abs[:], scalar1=SMALLEST, scalar2=None, op0=ALU.max)
+        nc.scalar.activation(out=inv_root[:], in_=t_safe[:], func=ACT.Abs_reciprocal_sqrt)
+        nc.gpsimd.tensor_scalar(out=t_step[:], in0=t_raw[:], scalar1=0.0, scalar2=2.0, op0=ALU.is_ge, op1=ALU.mult)
+        nc.gpsimd.tensor_scalar(out=t_sign[:], in0=t_step[:], scalar1=1.0, scalar2=-1.0, op0=ALU.mult, op1=ALU.add)
+        quantise(q_mx[0], 0, q_stage[0])
+        cast_first_keys(0)
+        nc.vector.tensor_tensor(out=root[:], in0=t_abs[:], in1=inv_root[:], op=ALU.mult)
+        quantise_first_keys(0)
+        nc.vector.scalar_tensor_tensor(out=newton[:], in0=root[:], scalar=-0.5, in1=inv_root[:], op0=ALU.mult, op1=ALU.mult)
+        cast_first_keys(1)
+        nc.vector.scalar_tensor_tensor(out=t_root[:], in0=newton[:], scalar=1.5, in1=root[:], op0=ALU.add, op1=ALU.mult)
+        quantise_first_keys(1)
         for g in range(H):
             scores(0, g)
         cast_q(1)
         cast_q(2)
-        cast_q(3)
-        quantize(q_mx[1], 0, q_stage[1][:])
+        quantise(q_mx[1], 0, q_stage[1])
 
-        def cast_second_k(piece):
-            half, pair = divmod(piece, 2)
-            dst = k_stage1[:].rearrange("p (r s j) -> p s j r", r=PACK, j=PACK)
-            nc.scalar.copy(
-                out=dst[:, half * (P // 2) : (half + 1) * (P // 2), :, 2 * pair : 2 * pair + 2], in_=k_src(2 + half, pair)
-            )
-
-        q_quantize_at = {1: 2, 5: 3}
-        scalar_reads = (2, 3, 4, 5, 6, 7)
-        first_y = 4
-        last = STEPS - 1
         for step in range(STEPS):
-            done = step - first_y
-            relu_scale(step, 0)
-            if step in scalar_reads:
-                relu_scale_on_scalar(step, 2)
-                if step < first_y:
+            b = step - FIRST_PRODUCT
+            scalar_reads = step >= SCALAR_READS_FROM
+            gpsimd_squares = FIRST_PRODUCT <= step < LAST
+            shared_stage_busy = FIRST_PRODUCT < step < LAST
+
+            read_scores(step, 0)
+            if scalar_reads:
+                read_scores_on_scalar(step)
+                if not gpsimd_squares:
                     square(step, 0, BANK)
-                else:
-                    if 2 <= done:
-                        normalise(done - 2, y_bank[done % 2], H)
-                        store(done - 2, done - 2, slice(0, H), H)
-                if step in (4, 5):
-                    square(2, (2 * step - 7) * BANK, BANK)
-                square_rows(step, 2)
-            if step in q_quantize_at:
-                quantize(q_mx[q_quantize_at[step]], 0, q_stage[q_quantize_at[step]][:])
-            if step < last and step != 2:
-                scores(step + 1, 0)
-            if step in (3, 4):
-                quantize(v_mx[step - 1], 0, v_stage[step - 3][:])
-            if step in (2, 3):
-                for c in range(NPASS):
-                    cast_v(step, c)
-            if step == 2:
-                quantize(k_mx[1], 0, k_stage1[:])
-                scores(step + 1, 0)
-            if 0 <= done < NQB - 1:
-                quantize_w(done, 0, H)
-            if done >= 1:
-                den_add(done - 1, y_bank[(done - 1) % 2], H)
-            if done == 0:
-                quantize_w(step - 1, 0, H)
-            if done >= 1:
-                quantize_w(step - 1, 1, 1)
-                quantize_w(step - 1, 2, 2)
-                den_rec(done - 1, H)
-                quantize(w_mx[step - 1], 0, q_stage[1][:])
-            if 1 <= step <= H:
-                quantize(v_mx[(step - 1) // 2], (step - 1) % 2 * D, q_stage[1][:])
-            if step < H:
-                cast_v_on_gpsimd(step // 2, step % 2)
-            else:
-                square_on_gpsimd(step)
-            if step in scalar_reads and step < last:
-                scores(step + 1, 2)
-            if 0 <= done < NQB - 1:
-                for g in range(H):
-                    second(done, g, y_bank[done % 2][:, g * D : (g + 1) * D], range(NPASS))
-            relu_scale(step, 1)
+                if b == 2:
+                    divide_on_scalar(0, y_bank[0], H)
+                    store(0, 0, slice(0, H), H)
+                if step in PUT_OFF:
+                    square(PUT_OFF_STEP, PUT_OFF[step] * BANK, BANK)
+                if not shared_stage_busy:
+                    square_places(step)
+
             if step == 1:
-                for piece in (1, 2, 3):
-                    cast_second_k(piece)
-            if step == 2:
-                pass
-            elif step in scalar_reads:
-                square(step, BANK, BANK)
-            else:
+                quantise(q_mx[2], 0, q_stage[2])
+            if step < LAST and step != SECOND_KEYS:
+                scores(step + 1, 0)
+            if step - 1 in (2, 3):
+                quantise(v_mx[step - 1], 0, v_stage[step - 3][:])
+            if step in (2, 3):
+                for c in range(PASSES):
+                    cast_v_on_vector(step, c)
+            if step == SECOND_KEYS:
+                quantise(k_mx[1], 0, k_second[:])
+                scores(step + 1, 0)
+            if 0 <= b < BLOCKS - 1:
+                quantise_w(ORDER.index((0, b)), 0, H)
+            if b >= 1:
+                denominators(b - 1, y_bank[(b - 1) % 2], H)
+            if step == LAST:
+                divide_on_vector(1, y_bank[1], H)
+                store(1, 1, slice(0, H), H)
+            if b >= 0:
+                quantise_w(step - 1, 0, H)
+            if b >= 1:
+                invert(b - 1, H)
+            if 1 <= step <= FIRST_PRODUCT:
+                quantise(v_mx[(step - 1) // PASSES], (step - 1) % PASSES * D, handover)
+
+            if step < FIRST_PRODUCT:
+                cast_v_on_gpsimd(step // PASSES, step % PASSES)
+            if gpsimd_squares:
+                square_by_product(nc.gpsimd, step, 0, BANK)
+
+            if scalar_reads and step < LAST:
+                scores(step + 1, SCALAR_HEAD)
+            if 0 <= b < BLOCKS - 1:
+                for g in range(H):
+                    second_product(b, g, y_bank[b % 2], g, range(PASSES))
+            if shared_stage_busy:
+                square_places(step)
+
+            read_scores(step, 1)
+            if step == 1:
+                for half, pair in ((0, 1), (1, 0), (1, 1)):
+                    cast_second_keys(half, pair)
+            if not scalar_reads:
                 square(step, 0, 2 * BANK)
-            if step < last:
+            elif step != PUT_OFF_STEP:
+                square(step, BANK, BANK)
+            if step < LAST:
                 scores(step + 1, 1)
-            if step not in scalar_reads:
-                relu_scale(step, 2)
+            if not scalar_reads:
+                read_scores(step, 2)
                 scores(step + 1, 2)
             if step == 0:
-                cast_second_k(0)
-            if step < last:
-                relu_scale(step, 3)
-                if step == 2:
-                    pass
-                elif step in scalar_reads:
-                    square(step, 3 * BANK, BANK)
-                else:
+                cast_second_keys(0, 0)
+            if step < LAST:
+                read_scores(step, 3)
+                if not scalar_reads:
                     square(step, 2 * BANK, 2 * BANK)
+                elif step != PUT_OFF_STEP:
+                    square(step, 3 * BANK, BANK)
                 scores(step + 1, 3)
 
-        b = NQB - 1
+        b = BLOCKS - 1
+        both, second, fourth = y_bank[2], y_bank[1], y_bank[3]
         for first in (0, QB // 2):
-            relu_scale(last, H - 1, first, QB // 2)
-            square(last, (H - 1) * BANK + first * PACK, BANK // 2)
-        second(b, 3, y_bank[3][:, 0:D], (0,))
-        normalise_on_vector(b - 1, y_bank[(b - 1) % 2], H)
+            read_scores(LAST, 3, first, QB // 2)
+        square(LAST, 3 * BANK, BANK // 2)
+        second_product(b, 3, fourth, 0, (0,))
+        second_product(b, 1, second, 0, (0,))
+        second_product(b, 0, both, 0, (0,))
+        quantise_w(LAST, 0, 1)
+        quantise_w(LAST, 2, 1)
+        square_by_product(nc.vector, LAST, 3 * BANK + BANK // 2, BANK // 2)
+        second_product(b, 0, both, 0, (1,))
+        second_product(b, 2, both, 1, range(PASSES))
+        divide_on_scalar(b - 1, y_bank[(b - 1) % 2], H)
         store(b - 1, b - 1, slice(0, H), H)
-        quantize_w(last, 2, 1)
-        quantize(w_mx[last], 0, q_stage[1][:])
-        quantize_w(last, 1, 1)
-        second(b, 2, y_bank[2][:, D : 2 * D], range(NPASS))
-        second(b, 0, y_bank[2][:, 0:D], range(NPASS))
-        second(b, 1, y_bank[1][:, 0:D], range(NPASS))
-        quantize_w(last, 3, 1)
-        second(b, 3, y_bank[3][:, 0:D], (1,))
-        den_add(b, y_bank[2], 2)
-        den_add(b + 1, y_bank[1], 1)
-        den_rec(b, 2)
-        den_rec(b + 1, 1)
-        den_add(b + 2, y_bank[3], 1)
-        normalise(b, y_bank[2], 2)
+        quantise_w(LAST, 1, 1)
+        quantise_w(LAST, 3, 1)
+        second_product(b, 1, second, 0, (1,))
+        second_product(b, 3, fourth, 0, (1,))
+        denominators(b, both, 2)
+        invert(b, 2)
+        denominators(b + 1, second, 1)
+        denominators(b + 2, fourth, 1)
+        divide_on_scalar(b, both, 2)
         store(b, b, slice(0, H, 2), 2)
-        den_rec(b + 2, 1)
-        normalise(b + 1, y_bank[1], 1)
+        invert(b + 1, 1)
+        invert(b + 2, 1)
+        divide_on_scalar(b + 1, second, 1)
+        divide_on_vector(b + 2, fourth, 1)
         store(b + 1, b, slice(1, 2), 1)
-        normalise_on_vector(b + 2, y_bank[3], 1)
         store(b + 2, b, slice(3, 4), 1)

from contextlib import ExitStack

import concourse.mybir as mybir

H, D, NQ, N = 4, 128, 512, 1024
FLOPS = 2 * 2 * H * D * NQ * N

F32 = mybir.dt.float32
BF16 = mybir.dt.bfloat16
U32 = mybir.dt.uint32
U8 = mybir.dt.uint8
FP8X4 = mybir.dt.float8_e4m3fn_x4
ALU = mybir.AluOpType
ACT = mybir.ActivationFunctionType

P = 128
PACK = 4
ROWS = D // PACK
QB = 128
BLOCKS = NQ // QB
PASS = P * PACK
PASSES = N // PASS
HALF = PASS // 2
BANK = PACK * QB
SMALLEST = 2.0**-126

ORDER = [(0, 0), (0, 1), (0, 2), (1, 0), (1, 1), (1, 2), (0, 3), (1, 3)]
STEPS = PASSES * BLOCKS
LAST = STEPS - 1
SECOND_KEYS = 2
FIRST_PRODUCT = 4
SCALAR_READS_FROM = 2
SCALAR_HEAD = 2
PUT_OFF_STEP = 2
PUT_OFF = {4: 1, 5: 3}


def tile_rows_relu2_kernel(tc, qT, kT, t, v, out):
    nc = tc.nc
    with ExitStack() as ctx:
        sbuf = ctx.enter_context(tc.tile_pool(name="sbuf", bufs=1))
        psum = ctx.enter_context(tc.psum_pool(name="psum", bufs=1))
        ctx.enter_context(tc.manual_schedule())

        def tiles(name, widths, dtype):
            return [sbuf.tile([P, w], dtype, name="%s%d" % (name, i), align_bytes=64) for i, w in enumerate(widths)]

        def quantised(name, widths):
            return list(zip(tiles(name + "_words", widths, U32), tiles(name + "_scales", widths, U8)))

        q_widths = [QB, QB, 2 * QB]
        q_raw = tiles("q_raw", [PACK * w for w in q_widths], F32)
        k_raw = tiles("k_raw", [PACK * HALF] * (N // HALF), F32)
        v_raw = tiles("v_raw", [PASSES * PACK * D] * H, F32)
        w_own = tiles("w_stage", [H * BANK] * (FIRST_PRODUCT + 1), BF16)
        w_stage = w_own + [w_own[FIRST_PRODUCT]] * (LAST - FIRST_PRODUCT - 1) + [w_own[FIRST_PRODUCT - 1]]
        handover = w_own[FIRST_PRODUCT][:, 0:BANK]
        q_first, q_rest = tiles("q_stage", [PACK * QB, PACK * 2 * QB], BF16)
        q_stage = [q_first[:], handover, q_rest[:]]
        k_first = tiles("k_first", [2 * HALF] * 4, BF16)
        k_second = tiles("k_second", [PACK * PASS], BF16)[0]
        v_stage = tiles("v_stage", [PASSES * PACK * D] * 2, BF16)
        x_words = tiles("x_words", [H * BANK] * STEPS, F32)
        x_places = tiles("x_places", [BANK] * 2, F32)
        q_mx = quantised("q", q_widths)
        k_mx = quantised("k", [PASS] * PASSES)
        v_mx = quantised("v", [PASSES * D] * H)
        w_mx = quantised("w", [H * QB] * STEPS)
        t_raw, t_abs, t_safe, inv_root, root, newton, t_root, t_step, t_sign = tiles("t", [PASSES * PACK] * 9, F32)
        groups = BLOCKS + 2
        den = tiles("den", [H] * groups, F32)
        inv_den = tiles("inv_den", [H] * groups, F32)
        result = tiles("result", [H * D] * groups, F32)
        score = [psum.tile([P, BANK], F32, name="score%d" % g) for g in range(H)]
        y_bank = [psum.tile([P, BANK], F32, name="y%d" % i) for i in range(4)]

        def rows_of(flat):
            return flat.rearrange("p (j n) -> p j n", j=PACK)

        def walk_rows(rows):
            return rows.rearrange("p j (u i) -> p u j i", i=PACK)

        def walk_words(flat):
            return flat.rearrange("p (u i j) -> p u j i", i=PACK, j=PACK)

        def token_values(column_tile, c):
            return column_tile[:, c * PACK : (c + 1) * PACK]

        def load_q(piece):
            first = sum(q_widths[:piece])
            source = qT.rearrange("h (p j) n -> (h p) j n", j=PACK)[:, :, first : first + q_widths[piece]]
            nc.sync.dma_start(out=rows_of(q_raw[piece][:]), in_=source)

        def load_k(half):
            source = kT.rearrange("h (p j) n -> (h p) j n", j=PACK)[:, :, half * HALF : (half + 1) * HALF]
            nc.sync.dma_start(out=rows_of(k_raw[half][:]), in_=source)

        def load_v(g):
            nc.sync.dma_start(
                out=v_raw[g][:].rearrange("p (c x) -> p c x", c=PASSES),
                in_=v[g].rearrange("(c p j) e -> p c (j e)", c=PASSES, j=PACK),
            )

        def cast_q(piece):
            nc.scalar.copy(out=walk_words(q_stage[piece]), in_=walk_rows(rows_of(q_raw[piece][:])))

        def k_tokens(half, pair):
            return k_raw[half][:].rearrange("p (j s r) -> p s j r", j=PACK, r=PACK)[:, :, :, 2 * pair : 2 * pair + 2]

        def cast_first_keys(half):
            dealt = [k_first[2 * half + pair][:].rearrange("p (r s j) -> p s j r", r=2, j=PACK) for pair in range(2)]
            nc.vector.tensor_copy(out=dealt[0], in_=k_tokens(half, 0))
            nc.scalar.copy(out=dealt[1], in_=k_tokens(half, 1))

        def quantise_first_keys(half):
            for r in range(PACK):
                stage = k_first[2 * half + r // 2][:, (r % 2) * HALF : (r % 2 + 1) * HALF]
                quantise(k_mx[0], r * P + half * (P // 2), stage)

        def cast_second_keys(half, pair):
            dealt = k_second[:].rearrange("p (r s j) -> p s j r", r=PACK, j=PACK)
            columns = slice(half * (P // 2), (half + 1) * (P // 2))
            nc.scalar.copy(out=dealt[:, columns, :, 2 * pair : 2 * pair + 2], in_=k_tokens(PASS // HALF + half, pair))

        def v_rows(g, c):
            return rows_of(v_raw[g][:, c * PACK * D : (c + 1) * PACK * D])

        def cast_v_on_vector(g, c):
            nc.vector.tensor_tensor(
                out=walk_words(v_stage[g - 2][:, c * PACK * D : (c + 1) * PACK * D]),
                in0=walk_rows(v_rows(g, c)),
                in1=token_values(t_sign, c).unsqueeze(1).unsqueeze(3).to_broadcast([P, D // PACK, PACK, PACK]),
                op=ALU.mult,
            )

        def cast_v_on_gpsimd(g, c):
            nc.gpsimd.tensor_tensor(
                out=handover.rearrange("p (e j) -> p e j", j=PACK),
                in0=v_rows(g, c).rearrange("p j e -> p e j"),
                in1=token_values(t_sign, c).unsqueeze(1).to_broadcast([P, D, PACK]),
                op=ALU.mult,
            )

        def quantise(target, first, stage):
            cols = slice(first, first + stage.shape[1] // PACK)
            nc.vector.quantize_mx(out=target[0][:, cols].bitcast(FP8X4), scales=target[1][:, cols], in_=stage)

        def quantise_w(step, first_head, heads):
            quantise(w_mx[step], first_head * QB, w_stage[step][:, first_head * BANK : (first_head + heads) * BANK])

        def matmul(dst, rows, lhs, lhs_first, rhs, rhs_first, start, stop):
            lhs_cols, rhs_cols = slice(lhs_first, lhs_first + P), slice(rhs_first, rhs_first + P)
            nc.tensor.matmul_mx(
                out=dst,
                lhsT=lhs[0][rows, lhs_cols].bitcast(FP8X4),
                lhsT_scale=lhs[1][rows, lhs_cols],
                rhs=rhs[0][rows, rhs_cols].bitcast(FP8X4),
                rhs_scale=rhs[1][rows, rhs_cols],
                start=start,
                stop=stop,
            )

        def scores(step, g):
            c, b = ORDER[step]
            piece = min(b, len(q_widths) - 1)
            rows = slice(ROWS * g, ROWS * (g + 1))
            for r in range(PACK):
                dst = score[g][:, r * QB : (r + 1) * QB]
                matmul(dst, rows, k_mx[c], r * P, q_mx[piece], (b - piece) * QB, True, True)

        def second_product(b, g, bank, slot, passes):
            for c in passes:
                dst = bank[:, slot * D : (slot + 1) * D]
                matmul(dst, slice(0, P), w_mx[ORDER.index((c, b))], g * QB, v_mx[g], c * D, c == 0, c == PASSES - 1)

        def read_scores(step, g, first=0, queries=QB):
            col = g * BANK + first * PACK
            nc.vector.scalar_tensor_tensor(
                out=x_words[step][:, col : col + queries * PACK].rearrange("p (n r) -> p n r", r=PACK),
                in0=score[g][:].rearrange("p (r n) -> p n r", r=PACK)[:, first : first + queries, :],
                scalar=0.0,
                in1=token_values(t_root, ORDER[step][0]).unsqueeze(1).to_broadcast([P, queries, PACK]),
                op0=ALU.max,
                op1=ALU.mult,
            )

        def read_scores_on_scalar(step):
            for r in range(PACK):
                cols = slice(r * QB, (r + 1) * QB)
                nc.scalar.activation(
                    out=x_places[step % 2][:, cols],
                    in_=score[SCALAR_HEAD][:, cols],
                    func=ACT.Relu,
                    scale=token_values(t_root, ORDER[step][0])[:, r : r + 1],
                )

        def square(step, first, width):
            cols = slice(first, first + width)
            nc.scalar.activation(out=w_stage[step][:, cols], in_=x_words[step][:, cols], func=ACT.Square)

        def square_places(step):
            nc.scalar.activation(
                out=walk_words(w_stage[step][:, SCALAR_HEAD * BANK : (SCALAR_HEAD + 1) * BANK]),
                in_=walk_rows(rows_of(x_places[step % 2][:])),
                func=ACT.Square,
            )

        def square_by_product(engine, step, first, width):
            x = x_words[step][:, first : first + width]
            engine.tensor_tensor(out=w_stage[step][:, first : first + width], in0=x, in1=x, op=ALU.mult)

        def by_head(flat, count):
            return flat[:, 0 : count * D].rearrange("p (g e) -> p g e", e=D)

        def denominators(group, bank, count):
            nc.vector.tensor_scalar(
                out=den[group][:, 0:count], in0=by_head(bank, count)[:, :, D - 1], scalar1=1.0, scalar2=None, op0=ALU.add
            )

        def invert(group, count):
            nc.vector.reciprocal(out=inv_den[group][:, 0:count], in_=den[group][:, 0:count])

        def divide_on_scalar(group, bank, count):
            for i in range(count):
                cols = slice(i * D, (i + 1) * D)
                nc.scalar.activation(
                    out=result[group][:, cols], in_=bank[:, cols], func=ACT.Copy, scale=inv_den[group][:, i : i + 1]
                )

        def divide_on_vector(group, bank, count):
            nc.vector.tensor_tensor(
                out=by_head(result[group], count),
                in0=by_head(bank, count),
                in1=inv_den[group][:, 0:count].unsqueeze(2).to_broadcast([P, count, D]),
                op=ALU.mult,
            )

        def store(group, b, heads, count):
            target = out[heads, b * QB : (b + 1) * QB, :].rearrange("g m e -> m g e")
            nc.sync.dma_start(out=target, in_=by_head(result[group], count))

        nc.scalar.dma_start(
            out=t_raw[:].rearrange("p (c j) -> p c j", c=PASSES), in_=t.rearrange("(c p j) o -> p c (j o)", c=PASSES, j=PACK)
        )
        load_q(0)
        load_k(0)
        load_k(1)
        load_q(1)
        load_q(2)
        load_v(0)
        load_k(2)
        load_k(3)
        for g in (2, 1, 3):
            load_v(g)

        nc.vector.tensor_copy(out=walk_words(q_stage[0]), in_=walk_rows(rows_of(q_raw[0][:])))
        nc.vector.scalar_tensor_tensor(out=t_abs[:], in0=t_raw[:], scalar=-1.0, in1=t_raw[:], op0=ALU.mult, op1=ALU.max)
        nc.vector.tensor_scalar(out=t_safe[:], in0=t_abs[:], scalar1=SMALLEST, scalar2=None, op0=ALU.max)
        nc.scalar.activation(out=inv_root[:], in_=t_safe[:], func=ACT.Abs_reciprocal_sqrt)
        nc.gpsimd.tensor_scalar(out=t_step[:], in0=t_raw[:], scalar1=0.0, scalar2=2.0, op0=ALU.is_ge, op1=ALU.mult)
        nc.gpsimd.tensor_scalar(out=t_sign[:], in0=t_step[:], scalar1=1.0, scalar2=-1.0, op0=ALU.mult, op1=ALU.add)
        quantise(q_mx[0], 0, q_stage[0])
        cast_first_keys(0)
        nc.vector.tensor_tensor(out=root[:], in0=t_abs[:], in1=inv_root[:], op=ALU.mult)
        quantise_first_keys(0)
        nc.vector.scalar_tensor_tensor(out=newton[:], in0=root[:], scalar=-0.5, in1=inv_root[:], op0=ALU.mult, op1=ALU.mult)
        cast_first_keys(1)
        nc.vector.scalar_tensor_tensor(out=t_root[:], in0=newton[:], scalar=1.5, in1=root[:], op0=ALU.add, op1=ALU.mult)
        quantise_first_keys(1)
        for g in range(H):
            scores(0, g)
        cast_q(1)
        cast_q(2)
        quantise(q_mx[1], 0, q_stage[1])

        for step in range(STEPS):
            b = step - FIRST_PRODUCT
            scalar_reads = step >= SCALAR_READS_FROM
            gpsimd_squares = FIRST_PRODUCT <= step < LAST
            shared_stage_busy = FIRST_PRODUCT < step < LAST

            read_scores(step, 0)
            if scalar_reads:
                read_scores_on_scalar(step)
                if not gpsimd_squares:
                    square(step, 0, BANK)
                if b == 2:
                    divide_on_scalar(0, y_bank[0], H)
                    store(0, 0, slice(0, H), H)
                if step in PUT_OFF:
                    square(PUT_OFF_STEP, PUT_OFF[step] * BANK, BANK)
                if not shared_stage_busy:
                    square_places(step)

            if step == 1:
                quantise(q_mx[2], 0, q_stage[2])
            if step < LAST and step != SECOND_KEYS:
                scores(step + 1, 0)
            if step - 1 in (2, 3):
                quantise(v_mx[step - 1], 0, v_stage[step - 3][:])
            if step in (2, 3):
                for c in range(PASSES):
                    cast_v_on_vector(step, c)
            if step == SECOND_KEYS:
                quantise(k_mx[1], 0, k_second[:])
                scores(step + 1, 0)
            if 0 <= b < BLOCKS - 1:
                quantise_w(ORDER.index((0, b)), 0, H)
            if b >= 1:
                denominators(b - 1, y_bank[(b - 1) % 2], H)
            if step == LAST:
                divide_on_vector(1, y_bank[1], H)
                store(1, 1, slice(0, H), H)
            if b >= 0:
                quantise_w(step - 1, 0, H)
            if b >= 1:
                invert(b - 1, H)
            if 1 <= step <= FIRST_PRODUCT:
                quantise(v_mx[(step - 1) // PASSES], (step - 1) % PASSES * D, handover)

            if step < FIRST_PRODUCT:
                cast_v_on_gpsimd(step // PASSES, step % PASSES)
            if gpsimd_squares:
                square_by_product(nc.gpsimd, step, 0, BANK)

            if scalar_reads and step < LAST:
                scores(step + 1, SCALAR_HEAD)
            if 0 <= b < BLOCKS - 1:
                for g in range(H):
                    second_product(b, g, y_bank[b % 2], g, range(PASSES))
            if shared_stage_busy:
                square_places(step)

            read_scores(step, 1)
            if step == 1:
                for half, pair in ((0, 1), (1, 0), (1, 1)):
                    cast_second_keys(half, pair)
            if not scalar_reads:
                square(step, 0, 2 * BANK)
            elif step != PUT_OFF_STEP:
                square(step, BANK, BANK)
            if step < LAST:
                scores(step + 1, 1)
            if not scalar_reads:
                read_scores(step, 2)
                scores(step + 1, 2)
            if step == 0:
                cast_second_keys(0, 0)
            if step < LAST:
                read_scores(step, 3)
                if not scalar_reads:
                    square(step, 2 * BANK, 2 * BANK)
                elif step != PUT_OFF_STEP:
                    square(step, 3 * BANK, BANK)
                scores(step + 1, 3)

        b = BLOCKS - 1
        both, second, fourth = y_bank[2], y_bank[1], y_bank[3]
        for first in (0, QB // 2):
            read_scores(LAST, 3, first, QB // 2)
        square(LAST, 3 * BANK, BANK // 2)
        second_product(b, 3, fourth, 0, (0,))
        second_product(b, 1, second, 0, (0,))
        second_product(b, 0, both, 0, (0,))
        quantise_w(LAST, 0, 1)
        quantise_w(LAST, 2, 1)
        square_by_product(nc.vector, LAST, 3 * BANK + BANK // 2, BANK // 2)
        second_product(b, 0, both, 0, (1,))
        second_product(b, 2, both, 1, range(PASSES))
        divide_on_scalar(b - 1, y_bank[(b - 1) % 2], H)
        store(b - 1, b - 1, slice(0, H), H)
        quantise_w(LAST, 1, 1)
        quantise_w(LAST, 3, 1)
        second_product(b, 1, second, 0, (1,))
        second_product(b, 3, fourth, 0, (1,))
        denominators(b, both, 2)
        invert(b, 2)
        denominators(b + 1, second, 1)
        denominators(b + 2, fourth, 1)
        divide_on_scalar(b, both, 2)
        store(b, b, slice(0, H, 2), 2)
        invert(b + 1, 1)
        invert(b + 2, 1)
        divide_on_scalar(b + 1, second, 1)
        divide_on_vector(b + 2, fourth, 1)
        store(b + 1, b, slice(1, 2), 1)
        store(b + 2, b, slice(3, 4), 1)
